import numpy as np
import ml_dtypes


def mxq(x, axis, fmt="e4m3"):
    dtype, down = {"e4m3": (ml_dtypes.float8_e4m3fn, 7), "e5m2": (ml_dtypes.float8_e5m2, 14)}[fmt]
    v = np.moveaxis(np.asarray(x, np.float32).astype(ml_dtypes.bfloat16).astype(np.float64), axis, -1)
    blocks = v.reshape(v.shape[:-1] + (-1, 32))
    amax = np.abs(blocks).max(-1, keepdims=True)
    byte = np.maximum(np.where(amax > 0, np.frexp(amax)[1] - 1 + 127, 0) - down, 1)
    scale = np.exp2(byte - 127.0)
    codes = (blocks / scale).astype(np.float32).astype(dtype).astype(np.float64)
    return np.moveaxis((codes * scale).reshape(v.shape), -1, axis)


WIDE = False


def mx_kscale(k):
    if not WIDE:
        return np.ones(k)
    levels = np.array([10, -10, 5, -5, 0])
    if k % 512:
        return np.exp2(np.random.permutation(np.resize(levels, k // 32))).repeat(32)
    a = np.empty((k // 512, 16))
    for p in range(k // 512):
        a[p, :8] = np.random.permutation(np.resize(levels, 8))
        for g in range(8):
            far = levels[np.abs(levels - a[p, g]) >= 10]
            a[p, g + 8] = far[np.random.randint(len(far))]
    return np.exp2(a.ravel()).repeat(32)


def f64(x):
    return np.asarray(x).astype(np.float64)


def striped(idx):
    return np.tile(idx.reshape(-1, 16).T, (8, 1)).astype(np.uint16)


def unstriped(offs):
    return offs[:16].T.reshape(-1).astype(np.int64)


def pack_weight(w):
    k, n = w.shape
    w = f64(np.asarray(w, np.float32).astype(ml_dtypes.bfloat16)).reshape(k // 32, 32, n)
    amax = np.abs(w).max(1)
    byte = np.clip(np.where(amax > 0, np.frexp(amax)[1] - 1 + 127 - 7, 1), 1, 254)
    scaled = (w * np.exp2(127.0 - byte)[:, None, :]).reshape(k, n).astype(np.float32)
    words = np.ascontiguousarray(scaled.reshape(k // 512, 128, 4, n).transpose(0, 1, 3, 2)).astype(ml_dtypes.float8_e4m3fn).view(np.uint8)
    return words, np.ascontiguousarray(byte.astype(np.uint8).reshape(k // 512, 16, n))


def unpack_weight(words, scales):
    g, p, n, _ = words.shape
    vals = np.ascontiguousarray(words).view(ml_dtypes.float8_e4m3fn).astype(np.float64) * np.repeat(np.exp2(scales.astype(np.float64) - 127.0), 8, axis=1)[..., None]
    return vals.transpose(0, 1, 3, 2).reshape(g * 512, n)


K, T, S, H, D, W, U = 512, 2048, 512, 512, 8, 2048, 1024
P = 2 ** 7


def setup_inputs():
    n = np.random.standard_normal
    s = mx_kscale(K)[:, None]
    u = mx_kscale(H)
    packed_xT = pack_weight(n((K, T)) * s)
    packed_eT = pack_weight(n((H, W)) / np.sqrt(H) / u[:, None])
    return {
        "x_words": packed_xT[0],
        "x_scales": packed_xT[1],
        "w1": (n((K, H)) / np.sqrt(K) / s * u).astype(np.float32),
        "e_words": packed_eT[0],
        "e_scales": packed_eT[1],
        "half": (np.tile(np.random.uniform(0.2, 1.0, W), (P, 1))).astype(np.float32),
        "own": (-np.random.uniform(0.2, 1.0, (S, 1))).astype(np.float32),
        "alpha": (np.tile(n(W), (P, 1))).astype(np.float32),
        "offs": striped(np.random.permutation(T)[:S]),
        "sv": striped(np.random.permutation(W)[:U]),
    }


def reference(x_words, x_scales, w1, e_words, e_scales, half, own, alpha, offs, sv):
    xq = unpack_weight(x_words, x_scales)[:, unstriped(offs)]
    h = mxq(f64(w1), 0, "e4m3").T @ xq
    e_sv = unpack_weight(e_words, e_scales)[:, unstriped(sv)]
    y = mxq(h, 0, "e4m3").T @ e_sv
    ee = np.exp(0.5 * y + f64(own) - (f64(half)[:1][:, unstriped(sv)]))
    gg = ee * (f64(alpha)[:1][:, unstriped(sv)])
    z = gg.reshape(len(gg), -1, D).sum(axis=2)
    return np.tanh(z)

@@ -1,0 +1,210 @@
+from contextlib import ExitStack
+
+import concourse.mybir as mybir
+
+K, T, S, H, D, W, U = 512, 2048, 512, 512, 8, 2048, 1024
+P = 128
+PACK = 4
+V = U // D
+TB = S // P
+FLOPS = 2 * K * H * S + 2 * H * S * U
+
+F32 = mybir.dt.float32
+BF16 = mybir.dt.bfloat16
+I32 = mybir.dt.int32
+U32 = mybir.dt.uint32
+U16 = mybir.dt.uint16
+U8 = mybir.dt.uint8
+FP8X4 = mybir.dt.float8_e4m3fn_x4
+ALU = mybir.AluOpType
+ACT = mybir.ActivationFunctionType
+
+ALPHA_ROW = 64
+GP_TILES = 5
+
+
+def load_scale_rows(nc, window, scales):
+    for r in range(4):
+        nc.sync.dma_start(out=window[r:P:32, :].bitcast(I32), in_=scales[0, r:16:4, :].bitcast(I32))
+
+
+def load_words(nc, window, words):
+    nc.sync.dma_start(out=window[:].bitcast(I32), in_=words[0].rearrange("p c r -> p (c r)").bitcast(I32))
+
+
+def tile_picked_yrbf_tanh_p_kernel(
+    tc, x_words, x_scales, w1, e_words, e_scales, half, own, alpha, offs, sv, out
+):
+    nc = tc.nc
+    with ExitStack() as ctx:
+        keep = ctx.enter_context(tc.tile_pool(name="keep", bufs=1))
+        work = ctx.enter_context(tc.tile_pool(name="work", bufs=8))
+        psum = ctx.enter_context(tc.psum_pool(name="psum", bufs=1))
+
+        def bank(b):
+            return psum.tile([P, 512], F32, name="bank%d" % b, tag="bank%d" % b)
+
+        offs_t = keep.tile([P, S // 16], U16)
+        sv_t = keep.tile([P, U // 16], U16)
+        xs_win = keep.tile([P, T], U8)
+        es_win = keep.tile([P, W], U8, tag="e_table")
+        ha_win = keep.tile([P, W], F32, tag="rows_then_w1_codes", align_bytes=64)
+        own_col = keep.tile([P, TB], F32)
+        diag = [keep.tile([P, P // 2], F32, name="diag", tag=tag) for tag in ("x_table", "w1")]
+        ident = keep.tile([P, P], F32)
+
+        nc.vector.memset(es_win[:].bitcast(I32), 0)
+        for g in range(2):
+            nc.gpsimd.iota(diag[g][:], [[1, P // 2]], base=g * (P // 2), channel_multiplier=-1, allow_small_or_imprecise_dtypes=True)
+            nc.gpsimd.tensor_scalar(ident[:, g * (P // 2) : (g + 1) * (P // 2)], diag[g][:], 0.0, None, ALU.is_equal)
+        nc.vector.memset(xs_win[:].bitcast(I32), 0)
+        nc.vector.memset(ha_win[:].bitcast(I32), 0)
+
+        nc.sync.dma_start(sv_t[:], sv)
+        nc.sync.dma_start(offs_t[:], offs)
+        nc.sync.dma_start(out=own_col[:], in_=own.rearrange("(p i) o -> p (i o)", i=TB))
+        load_scale_rows(nc, es_win, e_scales)
+        xw_win = keep.tile([P, T], U32, tag="x_table")
+        load_words(nc, xw_win, x_words)
+        load_scale_rows(nc, xs_win, x_scales)
+        nc.sync.dma_start(out=ha_win[0:1, :], in_=half[0:1, :])
+        nc.sync.dma_start(out=ha_win[ALPHA_ROW : ALPHA_ROW + 1, :], in_=alpha[0:1, :])
+
+        own_ps = bank(4)
+        for i in range(TB):
+            nc.tensor.transpose(own_ps[:, i * P : (i + 1) * P], own_col[:, i : i + 1].to_broadcast([P, P]), ident[:])
+        own_row = keep.tile([P, S], F32)
+        nc.scalar.copy(
+            out=own_row[:].rearrange("p (n i) -> p n i", i=TB), in_=own_ps[:].rearrange("p (i n) -> p n i", i=TB)
+        )
+        w_raw = keep.tile([P, PACK, H], F32, tag="w1")
+        w_rows = w1.rearrange("(p j) c -> p j c", j=PACK)
+        for g in range(2):
+            cols = slice(g * (H // 2), (g + 1) * (H // 2))
+            nc.sync.dma_start(out=w_raw[:, :, cols], in_=w_rows[:, :, cols])
+
+        es_g = keep.tile([P, U], U8, align_bytes=64)
+        es_d = keep.tile([P, U], U8, align_bytes=64)
+        xs_g = keep.tile([P, S], U8, align_bytes=64)
+        xw_g = keep.tile([P, S], U32, align_bytes=64)
+        ha_g = keep.tile([P, U], F32)
+        ew_d = keep.tile([P, U], U32, align_bytes=64)
+
+        def by_member(dst, src):
+            nc.vector.tensor_copy(
+                out=dst[:].rearrange("p (a b v) -> p a v b", a=2, b=4),
+                in_=src[:].rearrange("p (v a b) -> p a v b", a=2, b=4),
+            )
+
+        nc.vector.tensor_copy(es_g[:], es_win[:].indirect(sv_t[:]))
+        ew_win = keep.tile([P, W], U32, tag="e_table")
+        load_words(nc, ew_win, e_words)
+        by_member(es_d, es_g)
+        nc.vector.tensor_copy(xs_g[:], xs_win[:].indirect(offs_t[:]))
+        nc.vector.tensor_copy(xw_g[:], xw_win[:].indirect(offs_t[:]))
+        nc.vector.tensor_copy(ha_g[:], ha_win[:].indirect(sv_t[:]))
+
+        w_bf = keep.tile([P, PACK, P, PACK], BF16, align_bytes=64, tag="staging")
+        for g in range(2):
+            ms = slice(g * (P // 2), (g + 1) * (P // 2))
+            nc.scalar.copy(
+                out=w_bf[:].rearrange("p t m j -> p m j t")[:, ms],
+                in_=w_raw[:].rearrange("p j (m t) -> p m j t", t=PACK)[:, ms],
+            )
+        w_q = keep.tile([P, H], U32, align_bytes=64, tag="rows_then_w1_codes")
+        w_s = keep.tile([P, H], U8, align_bytes=64)
+        nc.vector.quantize_mx(out=w_q[:].bitcast(FP8X4), scales=w_s[:], in_=w_bf[:].rearrange("p t m j -> p (t m j)"))
+
+        ew_g = keep.tile([P, U], U32, align_bytes=64, tag="staging")
+        nc.vector.tensor_copy(ew_g[:], ew_win[:].indirect(sv_t[:]))
+        by_member(ew_d, ew_g)
+
+        h_bf = keep.tile([P, S, PACK], BF16, align_bytes=64)
+        for i in range(TB):
+            tok = slice(i * P, (i + 1) * P)
+            h_ps = bank(i)
+            for t in range(PACK):
+                col = slice(t * P, (t + 1) * P)
+                nc.tensor.matmul_mx(
+                    out=h_ps[:, col],
+                    lhsT=w_q[:, col].bitcast(FP8X4),
+                    lhsT_scale=w_s[:, col],
+                    rhs=xw_g[:, tok].bitcast(FP8X4),
+                    rhs_scale=xs_g[:, tok],
+                    start=True,
+                    stop=True,
+                )
+            nc.scalar.copy(out=h_bf[:, tok, :], in_=h_ps[:].rearrange("p (t n) -> p n t", t=PACK))
+        neg_half = keep.tile([P, D], F32)
+        coef = keep.tile([P, D], F32)
+        ha_d = ha_g[:].rearrange("p (v d) -> p d v", d=D)
+        for g in range(2):
+            ha_ps = bank(g)
+            for c in range(4):
+                nc.tensor.transpose(ha_ps[:, c * P : (c + 1) * P], ha_d[:, 4 * g + c, :], ident[:])
+            cols = ha_ps[:].rearrange("p (c r) -> p r c", c=4)
+            nc.scalar.activation(neg_half[:, 4 * g : 4 * g + 4], cols[:, 0, :], ACT.Copy, scale=-1.0)
+            nc.scalar.copy(coef[:, 4 * g : 4 * g + 4], cols[:, ALPHA_ROW, :])
+
+        h_q = keep.tile([P, S], U32, align_bytes=64, tag="staging")
+        h_s = keep.tile([P, S], U8, align_bytes=64)
+        nc.vector.quantize_mx(out=h_q[:].bitcast(FP8X4), scales=h_s[:], in_=h_bf[:].rearrange("p n t -> p (n t)"))
+
+        z_ps = [bank(i) for i in range(TB)]
+        y_ps = {}
+        gg = {}
+
+        def product(d):
+            col = slice(d * P, (d + 1) * P)
+            y_ps[d] = bank(4 + d % 4)
+            nc.tensor.matmul_mx(
+                out=y_ps[d][:],
+                lhsT=ew_d[:, col].bitcast(FP8X4),
+                lhsT_scale=es_d[:, col],
+                rhs=h_q[:].bitcast(FP8X4),
+                rhs_scale=h_s[:],
+                start=True,
+                stop=True,
+            )
+
+        def kernel_values(d):
+            arg = work.tile([P, S], F32)
+            nc.vector.scalar_tensor_tensor(arg[:], y_ps[d][:], 0.5, own_row[:], ALU.mult, ALU.add)
+            ee = work.tile([P, S], F32)
+            nc.scalar.activation(ee[:], arg[:], ACT.Exp, bias=neg_half[:, d : d + 1], scale=1.0)
+            return ee
+
+        def weigh(d, ee):
+            gg[d] = work.tile([P, S], F32, name="gg")
+            eng = nc.gpsimd if d < GP_TILES else nc.vector
+            eng.tensor_scalar(gg[d][:], ee[:], coef[:, d : d + 1], 0.0, ALU.mult, ALU.add)
+
+        def add_up(d):
+            for i in range(TB):
+                nc.tensor.matmul(
+                    z_ps[i][:, 0:V],
+                    lhsT=gg[d][:, i * P : (i + 1) * P],
+                    rhs=ident[:],
+                    start=(d == 0),
+                    stop=(d == D - 1),
+                    is_transpose=True,
+                )
+
+        for d in range(4):
+            product(d)
+        ees = []
+        for d in range(D):
+            ees.append(kernel_values(d))
+            if d + 4 < D:
+                product(d + 4)
+        for d in range(D):
+            weigh(d, ees[d])
+        for d in range(D):
+            add_up(d)
+
+        res = keep.tile([P, TB, V], F32)
+        for i in range(TB):
+            nc.scalar.activation(res[:, i, :], z_ps[i][:, 0:V], ACT.Tanh)
+        out_v = out.rearrange("(i p) v -> p i v", p=P)
+        for g in range(2):
+            nc.sync.dma_start(out=out_v[:, 2 * g : 2 * g + 2, :], in_=res[:, 2 * g : 2 * g + 2, :])

@@ -47,8 +47,8 @@ def tile_picked_yrbf_tanh_p_kernel(
         offs_t = keep.tile([P, S // 16], U16)
         sv_t = keep.tile([P, U // 16], U16)
         xs_win = keep.tile([P, T], U8)
-        es_win = keep.tile([P, W], U8, tag="e_table")
-        ha_win = keep.tile([P, W], F32, tag="rows_then_w1_codes", align_bytes=64)
+        es_win = keep.tile([P, W], U8, tag="e_table", align_bytes=64)
+        ha_win = keep.tile([P, W], F32, tag="rows_then_x_codes", align_bytes=64)
         own_col = keep.tile([P, TB], F32)
         diag = [keep.tile([P, P // 2], F32, name="diag", tag=tag) for tag in ("x_table", "w1")]
         ident = keep.tile([P, P], F32)
@@ -86,23 +86,19 @@ def tile_picked_yrbf_tanh_p_kernel(
         es_g = keep.tile([P, U], U8, align_bytes=64)
         es_d = keep.tile([P, U], U8, align_bytes=64)
         xs_g = keep.tile([P, S], U8, align_bytes=64)
-        xw_g = keep.tile([P, S], U32, align_bytes=64)
         ha_g = keep.tile([P, U], F32)
-        ew_d = keep.tile([P, U], U32, align_bytes=64)
 
-        def by_member(dst, src):
-            nc.vector.tensor_copy(
-                out=dst[:].rearrange("p (a b v) -> p a v b", a=2, b=4),
-                in_=src[:].rearrange("p (v a b) -> p a v b", a=2, b=4),
-            )
 
         nc.vector.tensor_copy(es_g[:], es_win[:].indirect(sv_t[:]))
-        ew_win = keep.tile([P, W], U32, tag="e_table")
+        ew_win = keep.tile([P, W], U32, tag="e_table", align_bytes=64)
         load_words(nc, ew_win, e_words)
-        by_member(es_d, es_g)
-        nc.vector.tensor_copy(xs_g[:], xs_win[:].indirect(offs_t[:]))
-        nc.vector.tensor_copy(xw_g[:], xw_win[:].indirect(offs_t[:]))
+        nc.vector.tensor_copy(
+            out=es_d[:].rearrange("p (d v) -> p d v", d=D), in_=es_g[:].rearrange("p (v d) -> p d v", d=D)
+        )
         nc.vector.tensor_copy(ha_g[:], ha_win[:].indirect(sv_t[:]))
+        nc.vector.tensor_copy(xs_g[:], xs_win[:].indirect(offs_t[:]))
+        xw_g = keep.tile([P, S], U32, align_bytes=64, tag="rows_then_x_codes")
+        nc.vector.tensor_copy(xw_g[:], xw_win[:].indirect(offs_t[:]))
 
         w_bf = keep.tile([P, PACK, P, PACK], BF16, align_bytes=64, tag="staging")
         for g in range(2):
@@ -111,15 +107,34 @@ def tile_picked_yrbf_tanh_p_kernel(
                 out=w_bf[:].rearrange("p t m j -> p m j t")[:, ms],
                 in_=w_raw[:].rearrange("p j (m t) -> p m j t", t=PACK)[:, ms],
             )
-        w_q = keep.tile([P, H], U32, align_bytes=64, tag="rows_then_w1_codes")
+        w_q = keep.tile([P, H], U32, align_bytes=64)
         w_s = keep.tile([P, H], U8, align_bytes=64)
         nc.vector.quantize_mx(out=w_q[:].bitcast(FP8X4), scales=w_s[:], in_=w_bf[:].rearrange("p t m j -> p (t m j)"))
 
         ew_g = keep.tile([P, U], U32, align_bytes=64, tag="staging")
         nc.vector.tensor_copy(ew_g[:], ew_win[:].indirect(sv_t[:]))
-        by_member(ew_d, ew_g)
+        ew_blocks = ew_g[:].rearrange("p (u w a b) -> p a u b w", a=2, b=4, w=4)
 
-        h_bf = keep.tile([P, S, PACK], BF16, align_bytes=64)
+        def deal_words(a, tag):
+            dealt = keep.tile([P, U // 2], U32, align_bytes=64, name="dealt", tag=tag)
+            nc.vector.tensor_copy(out=dealt[:].rearrange("p (b u w) -> p u b w", b=4, w=4), in_=ew_blocks[:, a])
+            return dealt
+
+        ew_d = [deal_words(0, "ew_low")]
+
+        member = keep.tile([P, 2, D], F32, tag="w1")
+        neg_half = member[:, 0, :]
+        coef = member[:, 1, :]
+        ha_d = ha_g[:].rearrange("p (v d) -> p d v", d=D)
+        for g in range(2):
+            ha_ps = bank(5 + g)
+            for c in range(4):
+                nc.tensor.transpose(ha_ps[:, c * P : (c + 1) * P], ha_d[:, 4 * g + c, :], ident[:])
+            cols = ha_ps[:].rearrange("p (c r) -> p r c", c=4)
+            nc.scalar.activation(neg_half[:, 4 * g : 4 * g + 4], cols[:, 0, :], ACT.Copy, scale=-1.0)
+            nc.scalar.copy(coef[:, 4 * g : 4 * g + 4], cols[:, ALPHA_ROW, :])
+
+        h_bf = keep.tile([P, S, PACK], BF16, align_bytes=64, tag="h_bf")
         for i in range(TB):
             tok = slice(i * P, (i + 1) * P)
             h_ps = bank(i)
@@ -135,51 +150,42 @@ def tile_picked_yrbf_tanh_p_kernel(
                     stop=True,
                 )
             nc.scalar.copy(out=h_bf[:, tok, :], in_=h_ps[:].rearrange("p (t n) -> p n t", t=PACK))
-        neg_half = keep.tile([P, D], F32)
-        coef = keep.tile([P, D], F32)
-        ha_d = ha_g[:].rearrange("p (v d) -> p d v", d=D)
-        for g in range(2):
-            ha_ps = bank(g)
-            for c in range(4):
-                nc.tensor.transpose(ha_ps[:, c * P : (c + 1) * P], ha_d[:, 4 * g + c, :], ident[:])
-            cols = ha_ps[:].rearrange("p (c r) -> p r c", c=4)
-            nc.scalar.activation(neg_half[:, 4 * g : 4 * g + 4], cols[:, 0, :], ACT.Copy, scale=-1.0)
-            nc.scalar.copy(coef[:, 4 * g : 4 * g + 4], cols[:, ALPHA_ROW, :])
-
-        h_q = keep.tile([P, S], U32, align_bytes=64, tag="staging")
+        h_q = keep.tile([P, S], U32, align_bytes=64, tag="e_table")
         h_s = keep.tile([P, S], U8, align_bytes=64)
         nc.vector.quantize_mx(out=h_q[:].bitcast(FP8X4), scales=h_s[:], in_=h_bf[:].rearrange("p n t -> p (n t)"))
 
-        z_ps = [bank(i) for i in range(TB)]
-        y_ps = {}
-        gg = {}
+        ew_d.append(deal_words(1, "h_bf"))
 
-        def product(d):
+        y_ps = []
+        for d in range(D):
             col = slice(d * P, (d + 1) * P)
-            y_ps[d] = bank(4 + d % 4)
+            y_ps.append(bank((4 + d) % 8))
             nc.tensor.matmul_mx(
                 out=y_ps[d][:],
-                lhsT=ew_d[:, col].bitcast(FP8X4),
+                lhsT=ew_d[d // 4][:, (d % 4) * P : (d % 4 + 1) * P].bitcast(FP8X4),
                 lhsT_scale=es_d[:, col],
                 rhs=h_q[:].bitcast(FP8X4),
                 rhs_scale=h_s[:],
                 start=True,
                 stop=True,
             )
-
-        def kernel_values(d):
+        whole = [slice(0, S)]
+        halves = [slice(0, S // 2), slice(S // 2, S)]
+        ee = []
+        for d in range(D):
             arg = work.tile([P, S], F32)
-            nc.vector.scalar_tensor_tensor(arg[:], y_ps[d][:], 0.5, own_row[:], ALU.mult, ALU.add)
-            ee = work.tile([P, S], F32)
-            nc.scalar.activation(ee[:], arg[:], ACT.Exp, bias=neg_half[:, d : d + 1], scale=1.0)
-            return ee
-
-        def weigh(d, ee):
-            gg[d] = work.tile([P, S], F32, name="gg")
+            ee.append(work.tile([P, S], F32, name="ee"))
+            for c in halves if d == D - 1 else whole:
+                nc.vector.scalar_tensor_tensor(arg[:, c], y_ps[d][:, c], 0.5, own_row[:, c], ALU.mult, ALU.add)
+                nc.scalar.activation(ee[d][:, c], arg[:, c], ACT.Exp, bias=neg_half[:, d : d + 1], scale=1.0)
+        gg = []
+        for d in range(D):
+            gg.append(work.tile([P, S], F32, name="gg"))
             eng = nc.gpsimd if d < GP_TILES else nc.vector
-            eng.tensor_scalar(gg[d][:], ee[:], coef[:, d : d + 1], 0.0, ALU.mult, ALU.add)
-
-        def add_up(d):
+            for c in halves if d == D - 1 else whole:
+                eng.tensor_scalar(gg[d][:, c], ee[d][:, c], coef[:, d : d + 1], 0.0, ALU.mult, ALU.add)
+        z_ps = [bank(4 + i) for i in range(TB)]
+        for d in range(D):
             for i in range(TB):
                 nc.tensor.matmul(
                     z_ps[i][:, 0:V],
@@ -189,18 +195,6 @@ def tile_picked_yrbf_tanh_p_kernel(
                     stop=(d == D - 1),
                     is_transpose=True,
                 )
-
-        for d in range(4):
-            product(d)
-        ees = []
-        for d in range(D):
-            ees.append(kernel_values(d))
-            if d + 4 < D:
-                product(d + 4)
-        for d in range(D):
-            weigh(d, ees[d])
-        for d in range(D):
-            add_up(d)
 
         res = keep.tile([P, TB, V], F32)
         for i in range(TB):

@@ -20,12 +20,12 @@ ALU = mybir.AluOpType
 ACT = mybir.ActivationFunctionType
 
 ALPHA_ROW = 64
-GP_TILES = 5
+GP_TILES = 4
 
 
-def load_scale_rows(nc, window, scales):
+def load_scale_rows(queue, window, scales):
     for r in range(4):
-        nc.sync.dma_start(out=window[r:P:32, :].bitcast(I32), in_=scales[0, r:16:4, :].bitcast(I32))
+        queue.dma_start(out=window[r:P:32, :].bitcast(I32), in_=scales[0, r:16:4, :].bitcast(I32))
 
 
 def load_words(nc, window, words):
@@ -38,7 +38,7 @@ def tile_picked_yrbf_tanh_p_kernel(
     nc = tc.nc
     with ExitStack() as ctx:
         keep = ctx.enter_context(tc.tile_pool(name="keep", bufs=1))
-        work = ctx.enter_context(tc.tile_pool(name="work", bufs=8))
+        work = ctx.enter_context(tc.tile_pool(name="work", bufs=12))
         psum = ctx.enter_context(tc.psum_pool(name="psum", bufs=1))
 
         def bank(b):
@@ -46,59 +46,59 @@ def tile_picked_yrbf_tanh_p_kernel(
 
         offs_t = keep.tile([P, S // 16], U16)
         sv_t = keep.tile([P, U // 16], U16)
-        xs_win = keep.tile([P, T], U8)
+        xs_win = keep.tile([P, T], U8, tag="x_scales", align_bytes=64)
         es_win = keep.tile([P, W], U8, tag="e_table", align_bytes=64)
-        ha_win = keep.tile([P, W], F32, tag="rows_then_x_codes", align_bytes=64)
-        own_col = keep.tile([P, TB], F32)
-        diag = [keep.tile([P, P // 2], F32, name="diag", tag=tag) for tag in ("x_table", "w1")]
-        ident = keep.tile([P, P], F32)
-
+        ha_win = keep.tile([P, W], F32, tag="rows", align_bytes=64)
+        zero = [keep.tile([P, 8], F32, name="zero", tag=tag, align_bytes=64) for tag in ("x_table", "diag", "w1")]
         nc.vector.memset(es_win[:].bitcast(I32), 0)
-        for g in range(2):
-            nc.gpsimd.iota(diag[g][:], [[1, P // 2]], base=g * (P // 2), channel_multiplier=-1, allow_small_or_imprecise_dtypes=True)
-            nc.gpsimd.tensor_scalar(ident[:, g * (P // 2) : (g + 1) * (P // 2)], diag[g][:], 0.0, None, ALU.is_equal)
+        for col in zero:
+            nc.vector.memset(col[:], 0.0)
+
+        def clear_rows(col, start, stop):
+            nc.vector.tensor_copy(ha_win[:, start:stop], col[:, 0:1].to_broadcast([P, stop - start]))
+
+        clear_rows(zero[0], 0, 256)
         nc.vector.memset(xs_win[:].bitcast(I32), 0)
-        nc.vector.memset(ha_win[:].bitcast(I32), 0)
+        clear_rows(zero[1], 256, 512)
+        clear_rows(zero[2], 512, W)
+        diag = keep.tile([P, P], F32, tag="diag", align_bytes=64)
+        ident = keep.tile([P, P], F32)
+        nc.gpsimd.iota(diag[:], [[1, P]], base=0, channel_multiplier=-1, allow_small_or_imprecise_dtypes=True)
+        nc.gpsimd.tensor_scalar(ident[:], diag[:], 0.0, None, ALU.is_equal)
 
         nc.sync.dma_start(sv_t[:], sv)
         nc.sync.dma_start(offs_t[:], offs)
+        own_col = keep.tile([P, TB], F32, tag="own", align_bytes=64)
         nc.sync.dma_start(out=own_col[:], in_=own.rearrange("(p i) o -> p (i o)", i=TB))
-        load_scale_rows(nc, es_win, e_scales)
-        xw_win = keep.tile([P, T], U32, tag="x_table")
+        load_scale_rows(nc.sync, es_win, e_scales)
+        xw_win = keep.tile([P, T], U32, tag="x_table", align_bytes=64)
         load_words(nc, xw_win, x_words)
-        load_scale_rows(nc, xs_win, x_scales)
         nc.sync.dma_start(out=ha_win[0:1, :], in_=half[0:1, :])
         nc.sync.dma_start(out=ha_win[ALPHA_ROW : ALPHA_ROW + 1, :], in_=alpha[0:1, :])
-
-        own_ps = bank(4)
-        for i in range(TB):
-            nc.tensor.transpose(own_ps[:, i * P : (i + 1) * P], own_col[:, i : i + 1].to_broadcast([P, P]), ident[:])
-        own_row = keep.tile([P, S], F32)
-        nc.scalar.copy(
-            out=own_row[:].rearrange("p (n i) -> p n i", i=TB), in_=own_ps[:].rearrange("p (i n) -> p n i", i=TB)
-        )
-        w_raw = keep.tile([P, PACK, H], F32, tag="w1")
+        load_scale_rows(nc.sync, xs_win, x_scales)
+        w_raw = keep.tile([P, PACK, H], F32, tag="w1", align_bytes=64)
         w_rows = w1.rearrange("(p j) c -> p j c", j=PACK)
         for g in range(2):
             cols = slice(g * (H // 2), (g + 1) * (H // 2))
             nc.sync.dma_start(out=w_raw[:, :, cols], in_=w_rows[:, :, cols])
 
         es_g = keep.tile([P, U], U8, align_bytes=64)
-        es_d = keep.tile([P, U], U8, align_bytes=64)
         xs_g = keep.tile([P, S], U8, align_bytes=64)
-        ha_g = keep.tile([P, U], F32)
-
 
         nc.vector.tensor_copy(es_g[:], es_win[:].indirect(sv_t[:]))
         ew_win = keep.tile([P, W], U32, tag="e_table", align_bytes=64)
         load_words(nc, ew_win, e_words)
-        nc.vector.tensor_copy(
-            out=es_d[:].rearrange("p (d v) -> p d v", d=D), in_=es_g[:].rearrange("p (v d) -> p d v", d=D)
-        )
+        ha_g = keep.tile([P, U], F32, align_bytes=64)
         nc.vector.tensor_copy(ha_g[:], ha_win[:].indirect(sv_t[:]))
-        nc.vector.tensor_copy(xs_g[:], xs_win[:].indirect(offs_t[:]))
-        xw_g = keep.tile([P, S], U32, align_bytes=64, tag="rows_then_x_codes")
+        xw_g = keep.tile([P, S], U32, align_bytes=64, tag="rows")
         nc.vector.tensor_copy(xw_g[:], xw_win[:].indirect(offs_t[:]))
+        nc.vector.tensor_copy(xs_g[:], xs_win[:].indirect(offs_t[:]))
+        es_members = es_g[:].rearrange("p (v d) -> p d v", d=D)
+
+        def deal_scales(a, tag):
+            dealt = keep.tile([P, U // 2], U8, align_bytes=64, name="dealt_scales", tag=tag)
+            nc.vector.tensor_copy(out=dealt[:].rearrange("p (d v) -> p d v", d=4), in_=es_members[:, 4 * a : 4 * a + 4, :])
+            return dealt
 
         w_bf = keep.tile([P, PACK, P, PACK], BF16, align_bytes=64, tag="staging")
         for g in range(2):
@@ -116,25 +116,14 @@ def tile_picked_yrbf_tanh_p_kernel(
         ew_blocks = ew_g[:].rearrange("p (u w a b) -> p a u b w", a=2, b=4, w=4)
 
         def deal_words(a, tag):
-            dealt = keep.tile([P, U // 2], U32, align_bytes=64, name="dealt", tag=tag)
+            dealt = keep.tile([P, U // 2], U32, align_bytes=64, name="dealt_words", tag=tag)
             nc.vector.tensor_copy(out=dealt[:].rearrange("p (b u w) -> p u b w", b=4, w=4), in_=ew_blocks[:, a])
             return dealt
 
+        es_d = [deal_scales(0, "e_table")]
         ew_d = [deal_words(0, "ew_low")]
 
-        member = keep.tile([P, 2, D], F32, tag="w1")
-        neg_half = member[:, 0, :]
-        coef = member[:, 1, :]
-        ha_d = ha_g[:].rearrange("p (v d) -> p d v", d=D)
-        for g in range(2):
-            ha_ps = bank(5 + g)
-            for c in range(4):
-                nc.tensor.transpose(ha_ps[:, c * P : (c + 1) * P], ha_d[:, 4 * g + c, :], ident[:])
-            cols = ha_ps[:].rearrange("p (c r) -> p r c", c=4)
-            nc.scalar.activation(neg_half[:, 4 * g : 4 * g + 4], cols[:, 0, :], ACT.Copy, scale=-1.0)
-            nc.scalar.copy(coef[:, 4 * g : 4 * g + 4], cols[:, ALPHA_ROW, :])
-
-        h_bf = keep.tile([P, S, PACK], BF16, align_bytes=64, tag="h_bf")
+        h_bf = [keep.tile([P, S // 2, PACK], BF16, align_bytes=64, name="h_bf", tag="h_bf%d" % g) for g in range(2)]
         for i in range(TB):
             tok = slice(i * P, (i + 1) * P)
             h_ps = bank(i)
@@ -149,26 +138,65 @@ def tile_picked_yrbf_tanh_p_kernel(
                     start=True,
                     stop=True,
                 )
-            nc.scalar.copy(out=h_bf[:, tok, :], in_=h_ps[:].rearrange("p (t n) -> p n t", t=PACK))
-        h_q = keep.tile([P, S], U32, align_bytes=64, tag="e_table")
+            nc.scalar.copy(out=h_bf[i // 2][:, (i % 2) * P : (i % 2 + 1) * P, :], in_=h_ps[:].rearrange("p (t n) -> p n t", t=PACK))
+
+        own_ps = bank(4)
+        for i in range(TB):
+            nc.tensor.transpose(own_ps[:, i * P : (i + 1) * P], own_col[:, i : i + 1].to_broadcast([P, P]), ident[:])
+        consts = keep.tile([P, S + 2 * D], F32, tag="w1", align_bytes=64)
+        own_row = consts[:, 0:S]
+        nc.scalar.copy(
+            out=own_row.rearrange("p (n i) -> p n i", i=TB), in_=own_ps[:].rearrange("p (i n) -> p n i", i=TB)
+        )
+
+        neg_half = consts[:, S : S + D]
+        coef = consts[:, S + D : S + 2 * D]
+        ha_d = ha_g[:].rearrange("p (v d) -> p d v", d=D)
+        for g in range(2):
+            ha_ps = bank(5 + g)
+            for c in range(4):
+                nc.tensor.transpose(ha_ps[:, c * P : (c + 1) * P], ha_d[:, 4 * g + c, :], ident[:])
+            cols = ha_ps[:].rearrange("p (c r) -> p r c", c=4)
+            nc.scalar.activation(neg_half[:, 4 * g : 4 * g + 4], cols[:, 0, :], ACT.Copy, scale=-1.0)
+            nc.scalar.copy(coef[:, 4 * g : 4 * g + 4], cols[:, ALPHA_ROW, :])
+
+        h_q = keep.tile([P, S], U32, align_bytes=64)
         h_s = keep.tile([P, S], U8, align_bytes=64)
-        nc.vector.quantize_mx(out=h_q[:].bitcast(FP8X4), scales=h_s[:], in_=h_bf[:].rearrange("p n t -> p (n t)"))
+        for g in range(2):
+            tok = slice(g * (S // 2), (g + 1) * (S // 2))
+            nc.vector.quantize_mx(out=h_q[:, tok].bitcast(FP8X4), scales=h_s[:, tok], in_=h_bf[g][:].rearrange("p n t -> p (n t)"))
+        ew_d.append(deal_words(1, "h_bf1"))
+        es_d.append(deal_scales(1, "staging"))
 
-        ew_d.append(deal_words(1, "h_bf"))
-
-        y_ps = []
-        for d in range(D):
-            col = slice(d * P, (d + 1) * P)
-            y_ps.append(bank((4 + d) % 8))
+        def second_product(d):
+            col = slice((d % 4) * P, (d % 4 + 1) * P)
+            y_ps = bank((4 + d) % 8)
             nc.tensor.matmul_mx(
-                out=y_ps[d][:],
-                lhsT=ew_d[d // 4][:, (d % 4) * P : (d % 4 + 1) * P].bitcast(FP8X4),
-                lhsT_scale=es_d[:, col],
+                out=y_ps[:],
+                lhsT=ew_d[d // 4][:, col].bitcast(FP8X4),
+                lhsT_scale=es_d[d // 4][:, col],
                 rhs=h_q[:].bitcast(FP8X4),
                 rhs_scale=h_s[:],
                 start=True,
                 stop=True,
             )
+            return y_ps
+
+        def weigh_and_add(eng, d, ee, blocks):
+            c = slice(blocks[0] * P, (blocks[-1] + 1) * P)
+            gg = work.tile([P, S], F32, name="gg")
+            eng.tensor_scalar(gg[:, c], ee[:, c], coef[:, d : d + 1], 0.0, ALU.mult, ALU.add)
+            for i in blocks:
+                nc.tensor.matmul(
+                    z_ps[i][:, 0:V],
+                    lhsT=gg[:, i * P : (i + 1) * P],
+                    rhs=ident[:],
+                    start=(d == 0),
+                    stop=(d == D - 1),
+                    is_transpose=True,
+                )
+
+        y_ps = [second_product(d) for d in range(D)]
         whole = [slice(0, S)]
         halves = [slice(0, S // 2), slice(S // 2, S)]
         ee = []
@@ -178,27 +206,16 @@ def tile_picked_yrbf_tanh_p_kernel(
             for c in halves if d == D - 1 else whole:
                 nc.vector.scalar_tensor_tensor(arg[:, c], y_ps[d][:, c], 0.5, own_row[:, c], ALU.mult, ALU.add)
                 nc.scalar.activation(ee[d][:, c], arg[:, c], ACT.Exp, bias=neg_half[:, d : d + 1], scale=1.0)
-        gg = []
-        for d in range(D):
-            gg.append(work.tile([P, S], F32, name="gg"))
-            eng = nc.gpsimd if d < GP_TILES else nc.vector
-            for c in halves if d == D - 1 else whole:
-                eng.tensor_scalar(gg[d][:, c], ee[d][:, c], coef[:, d : d + 1], 0.0, ALU.mult, ALU.add)
         z_ps = [bank(4 + i) for i in range(TB)]
-        for d in range(D):
-            for i in range(TB):
-                nc.tensor.matmul(
-                    z_ps[i][:, 0:V],
-                    lhsT=gg[d][:, i * P : (i + 1) * P],
-                    rhs=ident[:],
-                    start=(d == 0),
-                    stop=(d == D - 1),
-                    is_transpose=True,
-                )
+        for d in range(GP_TILES):
+            weigh_and_add(nc.gpsimd, d, ee[d], range(TB))
 
         res = keep.tile([P, TB, V], F32)
-        for i in range(TB):
-            nc.scalar.activation(res[:, i, :], z_ps[i][:, 0:V], ACT.Tanh)
         out_v = out.rearrange("(i p) v -> p i v", p=P)
         for g in range(2):
+            blocks = range(2 * g, 2 * g + 2)
+            for d in range(GP_TILES, D):
+                weigh_and_add(nc.vector, d, ee[d], blocks)
+            for i in blocks:
+                nc.scalar.activation(res[:, i, :], z_ps[i][:, 0:V], ACT.Tanh)
             nc.sync.dma_start(out=out_v[:, 2 * g : 2 * g + 2, :], in_=res[:, 2 * g : 2 * g + 2, :])

@@ -21,6 +21,8 @@ ACT = mybir.ActivationFunctionType
 
 ALPHA_ROW = 64
 GP_TILES = 4
+FIRST = 2
+KEEP_WARM = (4, 5, 6)
 
 
 def load_scale_rows(queue, window, scales):
@@ -38,7 +40,8 @@ def tile_picked_yrbf_tanh_p_kernel(
     nc = tc.nc
     with ExitStack() as ctx:
         keep = ctx.enter_context(tc.tile_pool(name="keep", bufs=1))
-        work = ctx.enter_context(tc.tile_pool(name="work", bufs=12))
+        work = ctx.enter_context(tc.tile_pool(name="work", bufs=14))
+        late = ctx.enter_context(tc.tile_pool(name="late", bufs=1))
         psum = ctx.enter_context(tc.psum_pool(name="psum", bufs=1))
 
         def bank(b):
@@ -46,10 +49,10 @@ def tile_picked_yrbf_tanh_p_kernel(
 
         offs_t = keep.tile([P, S // 16], U16)
         sv_t = keep.tile([P, U // 16], U16)
-        xs_win = keep.tile([P, T], U8, tag="x_scales", align_bytes=64)
-        es_win = keep.tile([P, W], U8, tag="e_table", align_bytes=64)
+        xs_win = keep.tile([P, T], U8, align_bytes=64)
+        es_win = late.tile([P, W], U8, align_bytes=64, offset=4 * U)
         ha_win = keep.tile([P, W], F32, tag="rows", align_bytes=64)
-        zero = [keep.tile([P, 8], F32, name="zero", tag=tag, align_bytes=64) for tag in ("x_table", "diag", "w1")]
+        zero = [keep.tile([P, 8], F32, name="zero", tag=tag, align_bytes=64) for tag in ("w1", "diag", "own", "x_table")]
         nc.vector.memset(es_win[:].bitcast(I32), 0)
         for col in zero:
             nc.vector.memset(col[:], 0.0)
@@ -60,7 +63,8 @@ def tile_picked_yrbf_tanh_p_kernel(
         clear_rows(zero[0], 0, 256)
         nc.vector.memset(xs_win[:].bitcast(I32), 0)
         clear_rows(zero[1], 256, 512)
-        clear_rows(zero[2], 512, W)
+        clear_rows(zero[3], 512, W - 256)
+        clear_rows(zero[2], W - 256, W)
         diag = keep.tile([P, P], F32, tag="diag", align_bytes=64)
         ident = keep.tile([P, P], F32)
         nc.gpsimd.iota(diag[:], [[1, P]], base=0, channel_multiplier=-1, allow_small_or_imprecise_dtypes=True)
@@ -68,39 +72,34 @@ def tile_picked_yrbf_tanh_p_kernel(
 
         nc.sync.dma_start(sv_t[:], sv)
         nc.sync.dma_start(offs_t[:], offs)
-        own_col = keep.tile([P, TB], F32, tag="own", align_bytes=64)
-        nc.sync.dma_start(out=own_col[:], in_=own.rearrange("(p i) o -> p (i o)", i=TB))
         load_scale_rows(nc.sync, es_win, e_scales)
-        xw_win = keep.tile([P, T], U32, tag="x_table", align_bytes=64)
-        load_words(nc, xw_win, x_words)
-        nc.sync.dma_start(out=ha_win[0:1, :], in_=half[0:1, :])
-        nc.sync.dma_start(out=ha_win[ALPHA_ROW : ALPHA_ROW + 1, :], in_=alpha[0:1, :])
-        load_scale_rows(nc.sync, xs_win, x_scales)
         w_raw = keep.tile([P, PACK, H], F32, tag="w1", align_bytes=64)
         w_rows = w1.rearrange("(p j) c -> p j c", j=PACK)
         for g in range(2):
             cols = slice(g * (H // 2), (g + 1) * (H // 2))
             nc.sync.dma_start(out=w_raw[:, :, cols], in_=w_rows[:, :, cols])
+        load_scale_rows(nc.sync, xs_win, x_scales)
+        xw_win = keep.tile([P, T], U32, tag="x_table", align_bytes=64)
+        load_words(nc, xw_win, x_words)
+        nc.sync.dma_start(out=ha_win[0:1, :], in_=half[0:1, :])
+        nc.sync.dma_start(out=ha_win[ALPHA_ROW : ALPHA_ROW + 1, :], in_=alpha[0:1, :])
+        own_col = keep.tile([P, TB], F32, tag="own", align_bytes=64)
+        nc.sync.dma_start(out=own_col[:], in_=own.rearrange("(p i) o -> p (i o)", i=TB))
 
         es_g = keep.tile([P, U], U8, align_bytes=64)
         xs_g = keep.tile([P, S], U8, align_bytes=64)
 
         nc.vector.tensor_copy(es_g[:], es_win[:].indirect(sv_t[:]))
-        ew_win = keep.tile([P, W], U32, tag="e_table", align_bytes=64)
+        ew_win = late.tile([P, W], U32, align_bytes=64, offset=4 * U)
         load_words(nc, ew_win, e_words)
-        ha_g = keep.tile([P, U], F32, align_bytes=64)
-        nc.vector.tensor_copy(ha_g[:], ha_win[:].indirect(sv_t[:]))
-        xw_g = keep.tile([P, S], U32, align_bytes=64, tag="rows")
-        nc.vector.tensor_copy(xw_g[:], xw_win[:].indirect(offs_t[:]))
         nc.vector.tensor_copy(xs_g[:], xs_win[:].indirect(offs_t[:]))
         es_members = es_g[:].rearrange("p (v d) -> p d v", d=D)
 
-        def deal_scales(a, tag):
-            dealt = keep.tile([P, U // 2], U8, align_bytes=64, name="dealt_scales", tag=tag)
-            nc.vector.tensor_copy(out=dealt[:].rearrange("p (d v) -> p d v", d=4), in_=es_members[:, 4 * a : 4 * a + 4, :])
-            return dealt
+        def deal_scales(members, dealt):
+            nc.vector.tensor_copy(out=dealt[:].rearrange("p (d v) -> p d v", v=V), in_=es_members[:, members, :])
+            return [dealt[:, d * V : (d + 1) * V] for d in range(members.stop - members.start)]
 
-        w_bf = keep.tile([P, PACK, P, PACK], BF16, align_bytes=64, tag="staging")
+        w_bf = keep.tile([P, PACK, P, PACK], BF16, align_bytes=64)
         for g in range(2):
             ms = slice(g * (P // 2), (g + 1) * (P // 2))
             nc.scalar.copy(
@@ -111,19 +110,22 @@ def tile_picked_yrbf_tanh_p_kernel(
         w_s = keep.tile([P, H], U8, align_bytes=64)
         nc.vector.quantize_mx(out=w_q[:].bitcast(FP8X4), scales=w_s[:], in_=w_bf[:].rearrange("p t m j -> p (t m j)"))
 
-        ew_g = keep.tile([P, U], U32, align_bytes=64, tag="staging")
+        xw_g = keep.tile([P, S], U32, align_bytes=64)
+        nc.vector.tensor_copy(xw_g[:], xw_win[:].indirect(offs_t[:]))
+        ha_g = keep.tile([P, U], F32, align_bytes=64)
+        nc.vector.tensor_copy(ha_g[:], ha_win[:].indirect(sv_t[:]))
+        ew_g = keep.tile([P, U], U32, align_bytes=64, tag="rows")
         nc.vector.tensor_copy(ew_g[:], ew_win[:].indirect(sv_t[:]))
-        ew_blocks = ew_g[:].rearrange("p (u w a b) -> p a u b w", a=2, b=4, w=4)
+        ew_members = ew_g[:].rearrange("p (u w d) -> p u d w", d=D, w=4)
 
-        def deal_words(a, tag):
-            dealt = keep.tile([P, U // 2], U32, align_bytes=64, name="dealt_words", tag=tag)
-            nc.vector.tensor_copy(out=dealt[:].rearrange("p (b u w) -> p u b w", b=4, w=4), in_=ew_blocks[:, a])
-            return dealt
+        def deal_words(members, dealt):
+            nc.vector.tensor_copy(out=dealt[:].rearrange("p (d u w) -> p u d w", w=4, u=V // 4), in_=ew_members[:, :, members, :])
+            return [dealt[:, d * V : (d + 1) * V] for d in range(members.stop - members.start)]
 
-        es_d = [deal_scales(0, "e_table")]
-        ew_d = [deal_words(0, "ew_low")]
+        es_d = deal_scales(slice(0, FIRST), late.tile([P, FIRST * V], U8, align_bytes=64, name="es_first", offset=6 * U))
+        ew_d = deal_words(slice(0, FIRST), keep.tile([P, FIRST * V], U32, align_bytes=64, name="ew_first"))
 
-        h_bf = [keep.tile([P, S // 2, PACK], BF16, align_bytes=64, name="h_bf", tag="h_bf%d" % g) for g in range(2)]
+        h_bf = late.tile([P, S, PACK], BF16, align_bytes=64, offset=0)
         for i in range(TB):
             tok = slice(i * P, (i + 1) * P)
             h_ps = bank(i)
@@ -138,7 +140,7 @@ def tile_picked_yrbf_tanh_p_kernel(
                     start=True,
                     stop=True,
                 )
-            nc.scalar.copy(out=h_bf[i // 2][:, (i % 2) * P : (i % 2 + 1) * P, :], in_=h_ps[:].rearrange("p (t n) -> p n t", t=PACK))
+            nc.scalar.copy(out=h_bf[:, tok, :], in_=h_ps[:].rearrange("p (t n) -> p n t", t=PACK))
 
         own_ps = bank(4)
         for i in range(TB):
@@ -153,28 +155,26 @@ def tile_picked_yrbf_tanh_p_kernel(
         coef = consts[:, S + D : S + 2 * D]
         ha_d = ha_g[:].rearrange("p (v d) -> p d v", d=D)
         for g in range(2):
-            ha_ps = bank(5 + g)
+            ha_ps = bank(2 + g)
             for c in range(4):
                 nc.tensor.transpose(ha_ps[:, c * P : (c + 1) * P], ha_d[:, 4 * g + c, :], ident[:])
             cols = ha_ps[:].rearrange("p (c r) -> p r c", c=4)
             nc.scalar.activation(neg_half[:, 4 * g : 4 * g + 4], cols[:, 0, :], ACT.Copy, scale=-1.0)
             nc.scalar.copy(coef[:, 4 * g : 4 * g + 4], cols[:, ALPHA_ROW, :])
 
-        h_q = keep.tile([P, S], U32, align_bytes=64)
+        h_q = late.tile([P, S], U32, align_bytes=64, offset=4 * U)
         h_s = keep.tile([P, S], U8, align_bytes=64)
-        for g in range(2):
-            tok = slice(g * (S // 2), (g + 1) * (S // 2))
-            nc.vector.quantize_mx(out=h_q[:, tok].bitcast(FP8X4), scales=h_s[:, tok], in_=h_bf[g][:].rearrange("p n t -> p (n t)"))
-        ew_d.append(deal_words(1, "h_bf1"))
-        es_d.append(deal_scales(1, "staging"))
+        nc.vector.quantize_mx(out=h_q[:].bitcast(FP8X4), scales=h_s[:], in_=h_bf[:].rearrange("p n t -> p (n t)"))
+        ew_d.extend(deal_words(slice(FIRST, 4), late.tile([P, (4 - FIRST) * V], U32, align_bytes=64, name="ew_second", offset=0)))
+        es_d.extend(deal_scales(slice(FIRST, D), late.tile([P, (D - FIRST) * V], U8, align_bytes=64, name="es_rest", offset=U)))
+        ew_d.extend(deal_words(slice(4, D), late.tile([P, 4 * V], U32, align_bytes=64, name="ew_high", offset=2 * U)))
 
         def second_product(d):
-            col = slice((d % 4) * P, (d % 4 + 1) * P)
             y_ps = bank((4 + d) % 8)
             nc.tensor.matmul_mx(
                 out=y_ps[:],
-                lhsT=ew_d[d // 4][:, col].bitcast(FP8X4),
-                lhsT_scale=es_d[d // 4][:, col],
+                lhsT=ew_d[d].bitcast(FP8X4),
+                lhsT_scale=es_d[d],
                 rhs=h_q[:].bitcast(FP8X4),
                 rhs_scale=h_s[:],
                 start=True,
@@ -206,6 +206,8 @@ def tile_picked_yrbf_tanh_p_kernel(
             for c in halves if d == D - 1 else whole:
                 nc.vector.scalar_tensor_tensor(arg[:, c], y_ps[d][:, c], 0.5, own_row[:, c], ALU.mult, ALU.add)
                 nc.scalar.activation(ee[d][:, c], arg[:, c], ACT.Exp, bias=neg_half[:, d : d + 1], scale=1.0)
+            if d in KEEP_WARM:
+                second_product(d)
         z_ps = [bank(4 + i) for i in range(TB)]
         for d in range(GP_TILES):
             weigh_and_add(nc.gpsimd, d, ee[d], range(TB))
@@ -214,8 +216,9 @@ def tile_picked_yrbf_tanh_p_kernel(
         out_v = out.rearrange("(i p) v -> p i v", p=P)
         for g in range(2):
             blocks = range(2 * g, 2 * g + 2)
-            for d in range(GP_TILES, D):
+            for d in range(GP_TILES, D - 1):
                 weigh_and_add(nc.vector, d, ee[d], blocks)
             for i in blocks:
+                weigh_and_add(nc.vector, D - 1, ee[D - 1], [i])
                 nc.scalar.activation(res[:, i, :], z_ps[i][:, 0:V], ACT.Tanh)
             nc.sync.dma_start(out=out_v[:, 2 * g : 2 * g + 2, :], in_=res[:, 2 * g : 2 * g + 2, :])

@@ -22,6 +22,7 @@ ACT = mybir.ActivationFunctionType
 ALPHA_ROW = 64
 GP_TILES = 4
 FIRST = 2
+E_ROW = P - 16
 KEEP_WARM = (4, 5, 6)
 
 
@@ -50,29 +51,32 @@ def tile_picked_yrbf_tanh_p_kernel(
         offs_t = keep.tile([P, S // 16], U16)
         sv_t = keep.tile([P, U // 16], U16)
         xs_win = keep.tile([P, T], U8, align_bytes=64)
-        es_win = late.tile([P, W], U8, align_bytes=64, offset=4 * U)
-        ha_win = keep.tile([P, W], F32, tag="rows", align_bytes=64)
-        zero = [keep.tile([P, 8], F32, name="zero", tag=tag, align_bytes=64) for tag in ("w1", "diag", "own", "x_table")]
-        nc.vector.memset(es_win[:].bitcast(I32), 0)
-        for col in zero:
-            nc.vector.memset(col[:], 0.0)
+        es_win = keep.tile([P, W], U8, align_bytes=64)
+        ha_win = keep.tile([P, W], F32, align_bytes=64)
+        zero = [keep.tile([P, 8], F32, name="zero", tag=tag, align_bytes=64) for tag in ("x_table", "diag", "own", "e_table")]
 
         def clear_rows(col, start, stop):
             nc.vector.tensor_copy(ha_win[:, start:stop], col[:, 0:1].to_broadcast([P, stop - start]))
 
-        clear_rows(zero[0], 0, 256)
+        nc.vector.memset(zero[0][:], 0.0)
         nc.vector.memset(xs_win[:].bitcast(I32), 0)
-        clear_rows(zero[1], 256, 512)
-        clear_rows(zero[3], 512, W - 256)
-        clear_rows(zero[2], W - 256, W)
+        clear_rows(zero[0], 0, 32)
+        for col in zero[1:]:
+            nc.vector.memset(col[:], 0.0)
+        nc.vector.memset(es_win[0:E_ROW, :].bitcast(I32), 0)
+        clear_rows(zero[1], 32, W - 64)
+        clear_rows(zero[2], W - 64, W - 32)
+        clear_rows(zero[3], W - 32, W)
         diag = keep.tile([P, P], F32, tag="diag", align_bytes=64)
         ident = keep.tile([P, P], F32)
         nc.gpsimd.iota(diag[:], [[1, P]], base=0, channel_multiplier=-1, allow_small_or_imprecise_dtypes=True)
         nc.gpsimd.tensor_scalar(ident[:], diag[:], 0.0, None, ALU.is_equal)
+        es_p = keep.tile([P, U], U8, align_bytes=64, tag="diag")
+        nc.gpsimd.memset(es_p[:].bitcast(I32), 0)
 
+        nc.sync.dma_start(out=es_win[E_ROW:P, :].bitcast(I32), in_=e_scales[0].bitcast(I32))
         nc.sync.dma_start(sv_t[:], sv)
         nc.sync.dma_start(offs_t[:], offs)
-        load_scale_rows(nc.sync, es_win, e_scales)
         w_raw = keep.tile([P, PACK, H], F32, tag="w1", align_bytes=64)
         w_rows = w1.rearrange("(p j) c -> p j c", j=PACK)
         for g in range(2):
@@ -85,15 +89,17 @@ def tile_picked_yrbf_tanh_p_kernel(
         nc.sync.dma_start(out=ha_win[ALPHA_ROW : ALPHA_ROW + 1, :], in_=alpha[0:1, :])
         own_col = keep.tile([P, TB], F32, tag="own", align_bytes=64)
         nc.sync.dma_start(out=own_col[:], in_=own.rearrange("(p i) o -> p (i o)", i=TB))
+        ew_win = keep.tile([P, W], U32, align_bytes=64, tag="e_table")
+        load_words(nc, ew_win, e_words)
 
-        es_g = keep.tile([P, U], U8, align_bytes=64)
+        es_g = keep.tile([P, U], U8, align_bytes=64, tag="e_scales")
         xs_g = keep.tile([P, S], U8, align_bytes=64)
 
         nc.vector.tensor_copy(es_g[:], es_win[:].indirect(sv_t[:]))
-        ew_win = late.tile([P, W], U32, align_bytes=64, offset=4 * U)
-        load_words(nc, ew_win, e_words)
+        for q in range(4):
+            nc.sync.dma_start(out=es_p[32 * q : 32 * q + 4, :].bitcast(I32), in_=es_g[E_ROW + 4 * q : E_ROW + 4 * q + 4, :].bitcast(I32))
         nc.vector.tensor_copy(xs_g[:], xs_win[:].indirect(offs_t[:]))
-        es_members = es_g[:].rearrange("p (v d) -> p d v", d=D)
+        es_members = es_p[:].rearrange("p (v d) -> p d v", d=D)
 
         def deal_scales(members, dealt):
             nc.vector.tensor_copy(out=dealt[:].rearrange("p (d v) -> p d v", v=V), in_=es_members[:, members, :])
@@ -112,18 +118,24 @@ def tile_picked_yrbf_tanh_p_kernel(
 
         xw_g = keep.tile([P, S], U32, align_bytes=64)
         nc.vector.tensor_copy(xw_g[:], xw_win[:].indirect(offs_t[:]))
+        es_d = deal_scales(slice(0, FIRST), keep.tile([P, FIRST * V], U8, align_bytes=64, name="es_first"))
         ha_g = keep.tile([P, U], F32, align_bytes=64)
         nc.vector.tensor_copy(ha_g[:], ha_win[:].indirect(sv_t[:]))
-        ew_g = keep.tile([P, U], U32, align_bytes=64, tag="rows")
-        nc.vector.tensor_copy(ew_g[:], ew_win[:].indirect(sv_t[:]))
+        ew_g = keep.tile([P, U], U32, align_bytes=64)
+        for g in range(2):
+            nc.vector.tensor_copy(ew_g[:, g * U // 2 : (g + 1) * U // 2], ew_win[:].indirect(sv_t[:, g * U // 32 : (g + 1) * U // 32]))
         ew_members = ew_g[:].rearrange("p (u w d) -> p u d w", d=D, w=4)
 
-        def deal_words(members, dealt):
-            nc.vector.tensor_copy(out=dealt[:].rearrange("p (d u w) -> p u d w", w=4, u=V // 4), in_=ew_members[:, :, members, :])
+        def deal_words(members, dealt, pieces=1):
+            for g in range(pieces):
+                us = slice(g * V // (4 * pieces), (g + 1) * V // (4 * pieces))
+                nc.vector.tensor_copy(
+                    out=dealt[:].rearrange("p (d u w) -> p u d w", w=4, u=V // 4)[:, us], in_=ew_members[:, us, members, :]
+                )
             return [dealt[:, d * V : (d + 1) * V] for d in range(members.stop - members.start)]
 
-        es_d = deal_scales(slice(0, FIRST), late.tile([P, FIRST * V], U8, align_bytes=64, name="es_first", offset=6 * U))
-        ew_d = deal_words(slice(0, FIRST), keep.tile([P, FIRST * V], U32, align_bytes=64, name="ew_first"))
+
+        ew_d = deal_words(slice(0, FIRST), keep.tile([P, FIRST * V], U32, align_bytes=64, name="ew_first"), pieces=2)
 
         h_bf = late.tile([P, S, PACK], BF16, align_bytes=64, offset=0)
         for i in range(TB):
@@ -162,7 +174,7 @@ def tile_picked_yrbf_tanh_p_kernel(
             nc.scalar.activation(neg_half[:, 4 * g : 4 * g + 4], cols[:, 0, :], ACT.Copy, scale=-1.0)
             nc.scalar.copy(coef[:, 4 * g : 4 * g + 4], cols[:, ALPHA_ROW, :])
 
-        h_q = late.tile([P, S], U32, align_bytes=64, offset=4 * U)
+        h_q = keep.tile([P, S], U32, align_bytes=64, tag="e_scales")
         h_s = keep.tile([P, S], U8, align_bytes=64)
         nc.vector.quantize_mx(out=h_q[:].bitcast(FP8X4), scales=h_s[:], in_=h_bf[:].rearrange("p n t -> p (n t)"))
         ew_d.extend(deal_words(slice(FIRST, 4), late.tile([P, (4 - FIRST) * V], U32, align_bytes=64, name="ew_second", offset=0)))

@@ -53,26 +53,25 @@ def tile_picked_yrbf_tanh_p_kernel(
         xs_win = keep.tile([P, T], U8, align_bytes=64)
         es_win = keep.tile([P, W], U8, align_bytes=64)
         ha_win = keep.tile([P, W], F32, align_bytes=64)
-        zero = [keep.tile([P, 8], F32, name="zero", tag=tag, align_bytes=64) for tag in ("x_table", "diag", "own", "e_table")]
+        zero = [keep.tile([P, 8], F32, name="zero", tag=tag, align_bytes=64) for tag in ("x_table", "own", "e_table")]
 
         def clear_rows(col, start, stop):
             nc.vector.tensor_copy(ha_win[:, start:stop], col[:, 0:1].to_broadcast([P, stop - start]))
 
+        diag = keep.tile([P, P], F32)
+        ident = keep.tile([P, P], F32)
+        es_p = keep.tile([P, U], U8, align_bytes=64)
+        nc.gpsimd.iota(diag[:], [[1, P]], base=0, channel_multiplier=-1, allow_small_or_imprecise_dtypes=True)
         nc.vector.memset(zero[0][:], 0.0)
         nc.vector.memset(xs_win[:].bitcast(I32), 0)
         clear_rows(zero[0], 0, 32)
         for col in zero[1:]:
             nc.vector.memset(col[:], 0.0)
         nc.vector.memset(es_win[0:E_ROW, :].bitcast(I32), 0)
-        clear_rows(zero[1], 32, W - 64)
-        clear_rows(zero[2], W - 64, W - 32)
-        clear_rows(zero[3], W - 32, W)
-        diag = keep.tile([P, P], F32, tag="diag", align_bytes=64)
-        ident = keep.tile([P, P], F32)
-        nc.gpsimd.iota(diag[:], [[1, P]], base=0, channel_multiplier=-1, allow_small_or_imprecise_dtypes=True)
-        nc.gpsimd.tensor_scalar(ident[:], diag[:], 0.0, None, ALU.is_equal)
-        es_p = keep.tile([P, U], U8, align_bytes=64, tag="diag")
-        nc.gpsimd.memset(es_p[:].bitcast(I32), 0)
+        clear_rows(zero[1], 32, W - 32)
+        clear_rows(zero[2], W - 32, W)
+        nc.vector.memset(es_p[:].bitcast(I32), 0)
+        nc.vector.tensor_scalar(ident[:], diag[:], 0.0, None, ALU.is_equal)
 
         nc.sync.dma_start(out=es_win[E_ROW:P, :].bitcast(I32), in_=e_scales[0].bitcast(I32))
         nc.sync.dma_start(sv_t[:], sv)
@@ -215,7 +214,7 @@ def tile_picked_yrbf_tanh_p_kernel(
         for d in range(D):
             arg = work.tile([P, S], F32)
             ee.append(work.tile([P, S], F32, name="ee"))
-            for c in halves if d == D - 1 else whole:
+            for c in halves if d in (0, D - 1) else whole:
                 nc.vector.scalar_tensor_tensor(arg[:, c], y_ps[d][:, c], 0.5, own_row[:, c], ALU.mult, ALU.add)
                 nc.scalar.activation(ee[d][:, c], arg[:, c], ACT.Exp, bias=neg_half[:, d : d + 1], scale=1.0)
             if d in KEEP_WARM:
@@ -233,4 +232,4 @@ def tile_picked_yrbf_tanh_p_kernel(
             for i in blocks:
                 weigh_and_add(nc.vector, D - 1, ee[D - 1], [i])
                 nc.scalar.activation(res[:, i, :], z_ps[i][:, 0:V], ACT.Tanh)
-            nc.sync.dma_start(out=out_v[:, 2 * g : 2 * g + 2, :], in_=res[:, 2 * g : 2 * g + 2, :])
+                nc.sync.dma_start(out=out_v[:, i, :], in_=res[:, i, :])

@@ -42,7 +42,7 @@ def tile_picked_yrbf_tanh_p_kernel(
     with ExitStack() as ctx:
         keep = ctx.enter_context(tc.tile_pool(name="keep", bufs=1))
         work = ctx.enter_context(tc.tile_pool(name="work", bufs=14))
-        late = ctx.enter_context(tc.tile_pool(name="late", bufs=1))
+        after_moves = ctx.enter_context(tc.tile_pool(name="after_moves", bufs=1))
         psum = ctx.enter_context(tc.psum_pool(name="psum", bufs=1))
 
         def bank(b):
@@ -91,7 +91,7 @@ def tile_picked_yrbf_tanh_p_kernel(
         ew_win = keep.tile([P, W], U32, align_bytes=64, tag="e_table")
         load_words(nc, ew_win, e_words)
 
-        es_g = keep.tile([P, U], U8, align_bytes=64, tag="e_scales")
+        es_g = after_moves.tile([P, U], U8, align_bytes=64, offset=4 * S)
         xs_g = keep.tile([P, S], U8, align_bytes=64)
 
         nc.vector.tensor_copy(es_g[:], es_win[:].indirect(sv_t[:]))
@@ -136,7 +136,7 @@ def tile_picked_yrbf_tanh_p_kernel(
 
         ew_d = deal_words(slice(0, FIRST), keep.tile([P, FIRST * V], U32, align_bytes=64, name="ew_first"), pieces=2)
 
-        h_bf = late.tile([P, S, PACK], BF16, align_bytes=64, offset=0)
+        h_bf = keep.tile([P, S, PACK], BF16, align_bytes=64, tag="h_bf")
         for i in range(TB):
             tok = slice(i * P, (i + 1) * P)
             h_ps = bank(i)
@@ -173,21 +173,23 @@ def tile_picked_yrbf_tanh_p_kernel(
             nc.scalar.activation(neg_half[:, 4 * g : 4 * g + 4], cols[:, 0, :], ACT.Copy, scale=-1.0)
             nc.scalar.copy(coef[:, 4 * g : 4 * g + 4], cols[:, ALPHA_ROW, :])
 
-        h_q = keep.tile([P, S], U32, align_bytes=64, tag="e_scales")
+        h_q = after_moves.tile([P, S], U32, align_bytes=64, offset=64)
         h_s = keep.tile([P, S], U8, align_bytes=64)
-        nc.vector.quantize_mx(out=h_q[:].bitcast(FP8X4), scales=h_s[:], in_=h_bf[:].rearrange("p n t -> p (n t)"))
-        ew_d.extend(deal_words(slice(FIRST, 4), late.tile([P, (4 - FIRST) * V], U32, align_bytes=64, name="ew_second", offset=0)))
-        es_d.extend(deal_scales(slice(FIRST, D), late.tile([P, (D - FIRST) * V], U8, align_bytes=64, name="es_rest", offset=U)))
-        ew_d.extend(deal_words(slice(4, D), late.tile([P, 4 * V], U32, align_bytes=64, name="ew_high", offset=2 * U)))
+        halves = [slice(0, S // 2), slice(S // 2, S)]
+        for c in halves:
+            nc.vector.quantize_mx(out=h_q[:, c].bitcast(FP8X4), scales=h_s[:, c], in_=h_bf[:, c, :].rearrange("p n t -> p (n t)"))
+        ew_d.extend(deal_words(slice(FIRST, 4), after_moves.tile([P, (4 - FIRST) * V], U32, align_bytes=64, name="ew_second", offset=4 * S + 64 + (D - FIRST) * V)))
+        es_d.extend(deal_scales(slice(FIRST, D), after_moves.tile([P, (D - FIRST) * V], U8, align_bytes=64, name="es_rest", offset=4 * S + 64)))
+        ew_d.extend(deal_words(slice(4, D), keep.tile([P, 4 * V], U32, align_bytes=64, name="ew_high", tag="h_bf")))
 
-        def second_product(d):
-            y_ps = bank((4 + d) % 8)
+        def second_product(d, c, b):
+            y_ps = bank(b)
             nc.tensor.matmul_mx(
-                out=y_ps[:],
+                out=y_ps[:, c],
                 lhsT=ew_d[d].bitcast(FP8X4),
                 lhsT_scale=es_d[d],
-                rhs=h_q[:].bitcast(FP8X4),
-                rhs_scale=h_s[:],
+                rhs=h_q[:, c].bitcast(FP8X4),
+                rhs_scale=h_s[:, c],
                 start=True,
                 stop=True,
             )
@@ -207,18 +209,21 @@ def tile_picked_yrbf_tanh_p_kernel(
                     is_transpose=True,
                 )
 
-        y_ps = [second_product(d) for d in range(D)]
-        whole = [slice(0, S)]
-        halves = [slice(0, S // 2), slice(S // 2, S)]
+        whole = slice(0, S)
+        first = [second_product(0, c, b) for c, b in zip(halves, (4, 3))]
+        y_ps = [None] + [second_product(d, whole, (4 + d) % 8) for d in range(1, D - 1)]
         ee = []
         for d in range(D):
             arg = work.tile([P, S], F32)
             ee.append(work.tile([P, S], F32, name="ee"))
-            for c in halves if d in (0, D - 1) else whole:
-                nc.vector.scalar_tensor_tensor(arg[:, c], y_ps[d][:, c], 0.5, own_row[:, c], ALU.mult, ALU.add)
-                nc.scalar.activation(ee[d][:, c], arg[:, c], ACT.Exp, bias=neg_half[:, d : d + 1], scale=1.0)
+            for g, c in enumerate(halves if d in (0, D - 1) else [whole]):
+                y = first[g] if d == 0 else y_ps[d]
+                nc.vector.scalar_tensor_tensor(arg[:, c], own_row[:, c], 2.0, y[:, c], ALU.mult, ALU.add)
+                nc.scalar.activation(ee[d][:, c], arg[:, c], ACT.Exp, bias=neg_half[:, d : d + 1], scale=0.5)
+            if d == 0:
+                y_ps.append(second_product(D - 1, whole, 3))
             if d in KEEP_WARM:
-                second_product(d)
+                second_product(d, whole, (4 + d) % 8)
         z_ps = [bank(4 + i) for i in range(TB)]
         for d in range(GP_TILES):
             weigh_and_add(nc.gpsimd, d, ee[d], range(TB))

@@ -19,7 +19,7 @@ FP8X4 = mybir.dt.float8_e4m3fn_x4
 ALU = mybir.AluOpType
 ACT = mybir.ActivationFunctionType
 
-ALPHA_ROW = 64
+HALF_ROW, ALPHA_ROW = P - 2, P - 1
 GP_TILES = 4
 FIRST = 2
 E_ROW = P - 16
@@ -53,28 +53,25 @@ def tile_picked_yrbf_tanh_p_kernel(
         xs_win = keep.tile([P, T], U8, align_bytes=64)
         es_win = keep.tile([P, W], U8, align_bytes=64)
         ha_win = keep.tile([P, W], F32, align_bytes=64)
-        zero = [keep.tile([P, 8], F32, name="zero", tag=tag, align_bytes=64) for tag in ("x_table", "own", "e_table")]
-
-        def clear_rows(col, start, stop):
-            nc.vector.tensor_copy(ha_win[:, start:stop], col[:, 0:1].to_broadcast([P, stop - start]))
+        zero = keep.tile([P, 8], F32, align_bytes=64)
 
         diag = keep.tile([P, P], F32)
         ident = keep.tile([P, P], F32)
         es_p = keep.tile([P, U], U8, align_bytes=64)
         nc.gpsimd.iota(diag[:], [[1, P]], base=0, channel_multiplier=-1, allow_small_or_imprecise_dtypes=True)
-        nc.vector.memset(zero[0][:], 0.0)
+        nc.vector.memset(zero[:], 0.0)
         nc.vector.memset(xs_win[:].bitcast(I32), 0)
-        clear_rows(zero[0], 0, 32)
-        for col in zero[1:]:
-            nc.vector.memset(col[:], 0.0)
         nc.vector.memset(es_win[0:E_ROW, :].bitcast(I32), 0)
-        clear_rows(zero[1], 32, W - 32)
-        clear_rows(zero[2], W - 32, W)
+        zero_rows = zero[0:HALF_ROW, 0:1].to_broadcast([HALF_ROW, W // 2])
+        nc.vector.tensor_copy(ha_win[0:HALF_ROW, 0 : W // 2], zero_rows)
+        nc.scalar.copy(ha_win[0:HALF_ROW, W // 2 : W], zero_rows)
         nc.vector.memset(es_p[:].bitcast(I32), 0)
         nc.vector.tensor_scalar(ident[:], diag[:], 0.0, None, ALU.is_equal)
 
         nc.sync.dma_start(out=es_win[E_ROW:P, :].bitcast(I32), in_=e_scales[0].bitcast(I32))
         nc.sync.dma_start(sv_t[:], sv)
+        nc.sync.dma_start(out=ha_win[HALF_ROW : HALF_ROW + 1, :], in_=half[0:1, :])
+        nc.sync.dma_start(out=ha_win[ALPHA_ROW : ALPHA_ROW + 1, :], in_=alpha[0:1, :])
         nc.sync.dma_start(offs_t[:], offs)
         w_raw = keep.tile([P, PACK, H], F32, tag="w1", align_bytes=64)
         w_rows = w1.rearrange("(p j) c -> p j c", j=PACK)
@@ -84,8 +81,6 @@ def tile_picked_yrbf_tanh_p_kernel(
         load_scale_rows(nc.sync, xs_win, x_scales)
         xw_win = keep.tile([P, T], U32, tag="x_table", align_bytes=64)
         load_words(nc, xw_win, x_words)
-        nc.sync.dma_start(out=ha_win[0:1, :], in_=half[0:1, :])
-        nc.sync.dma_start(out=ha_win[ALPHA_ROW : ALPHA_ROW + 1, :], in_=alpha[0:1, :])
         own_col = keep.tile([P, TB], F32, tag="own", align_bytes=64)
         nc.sync.dma_start(out=own_col[:], in_=own.rearrange("(p i) o -> p (i o)", i=TB))
         ew_win = keep.tile([P, W], U32, align_bytes=64, tag="e_table")
@@ -97,6 +92,8 @@ def tile_picked_yrbf_tanh_p_kernel(
         nc.vector.tensor_copy(es_g[:], es_win[:].indirect(sv_t[:]))
         for q in range(4):
             nc.sync.dma_start(out=es_p[32 * q : 32 * q + 4, :].bitcast(I32), in_=es_g[E_ROW + 4 * q : E_ROW + 4 * q + 4, :].bitcast(I32))
+        ha_g = keep.tile([P, U], F32, align_bytes=64)
+        nc.vector.tensor_copy(ha_g[:, 0 : U // 2], ha_win[:].indirect(sv_t[:, 0 : U // 32]))
         nc.vector.tensor_copy(xs_g[:], xs_win[:].indirect(offs_t[:]))
         es_members = es_p[:].rearrange("p (v d) -> p d v", d=D)
 
@@ -118,8 +115,11 @@ def tile_picked_yrbf_tanh_p_kernel(
         xw_g = keep.tile([P, S], U32, align_bytes=64)
         nc.vector.tensor_copy(xw_g[:], xw_win[:].indirect(offs_t[:]))
         es_d = deal_scales(slice(0, FIRST), keep.tile([P, FIRST * V], U8, align_bytes=64, name="es_first"))
-        ha_g = keep.tile([P, U], F32, align_bytes=64)
-        nc.vector.tensor_copy(ha_g[:], ha_win[:].indirect(sv_t[:]))
+        nc.vector.tensor_copy(ha_g[:, U // 2 : U], ha_win[:].indirect(sv_t[:, U // 32 : U // 16]))
+        half_col = keep.tile([P, D], F32, align_bytes=64)
+        coef = keep.tile([P, D], F32, align_bytes=64)
+        nc.sync.dma_start(out=half_col[:], in_=ha_g[HALF_ROW : HALF_ROW + 1, :])
+        nc.sync.dma_start(out=coef[:], in_=ha_g[ALPHA_ROW : ALPHA_ROW + 1, :])
         ew_g = keep.tile([P, U], U32, align_bytes=64)
         for g in range(2):
             nc.vector.tensor_copy(ew_g[:, g * U // 2 : (g + 1) * U // 2], ew_win[:].indirect(sv_t[:, g * U // 32 : (g + 1) * U // 32]))
@@ -163,15 +163,7 @@ def tile_picked_yrbf_tanh_p_kernel(
         )
 
         neg_half = consts[:, S : S + D]
-        coef = consts[:, S + D : S + 2 * D]
-        ha_d = ha_g[:].rearrange("p (v d) -> p d v", d=D)
-        for g in range(2):
-            ha_ps = bank(2 + g)
-            for c in range(4):
-                nc.tensor.transpose(ha_ps[:, c * P : (c + 1) * P], ha_d[:, 4 * g + c, :], ident[:])
-            cols = ha_ps[:].rearrange("p (c r) -> p r c", c=4)
-            nc.scalar.activation(neg_half[:, 4 * g : 4 * g + 4], cols[:, 0, :], ACT.Copy, scale=-1.0)
-            nc.scalar.copy(coef[:, 4 * g : 4 * g + 4], cols[:, ALPHA_ROW, :])
+        nc.scalar.activation(neg_half, half_col[:], ACT.Copy, scale=-1.0)
 
         h_q = after_moves.tile([P, S], U32, align_bytes=64, offset=64)
         h_s = keep.tile([P, S], U8, align_bytes=64)

@@ -66,7 +66,9 @@ def tile_picked_yrbf_tanh_p_kernel(
         nc.vector.tensor_copy(ha_win[0:HALF_ROW, 0 : W // 2], zero_rows)
         nc.scalar.copy(ha_win[0:HALF_ROW, W // 2 : W], zero_rows)
         nc.vector.memset(es_p[:].bitcast(I32), 0)
-        nc.vector.tensor_scalar(ident[:], diag[:], 0.0, None, ALU.is_equal)
+        diag_sq = keep.tile([P, P], F32)
+        nc.scalar.activation(diag_sq[:], diag[:], ACT.Square)
+        nc.scalar.activation(ident[:], diag_sq[:], ACT.Relu, bias=1.0, scale=-1.0)
 
         nc.sync.dma_start(out=es_win[E_ROW:P, :].bitcast(I32), in_=e_scales[0].bitcast(I32))
         nc.sync.dma_start(sv_t[:], sv)
@@ -79,10 +81,10 @@ def tile_picked_yrbf_tanh_p_kernel(
             cols = slice(g * (H // 2), (g + 1) * (H // 2))
             nc.sync.dma_start(out=w_raw[:, :, cols], in_=w_rows[:, :, cols])
         load_scale_rows(nc.sync, xs_win, x_scales)
-        xw_win = keep.tile([P, T], U32, tag="x_table", align_bytes=64)
-        load_words(nc, xw_win, x_words)
         own_col = keep.tile([P, TB], F32, tag="own", align_bytes=64)
         nc.sync.dma_start(out=own_col[:], in_=own.rearrange("(p i) o -> p (i o)", i=TB))
+        xw_win = keep.tile([P, T], U32, tag="x_table", align_bytes=64)
+        load_words(nc, xw_win, x_words)
         ew_win = keep.tile([P, W], U32, align_bytes=64, tag="e_table")
         load_words(nc, ew_win, e_words)
 
@@ -93,7 +95,7 @@ def tile_picked_yrbf_tanh_p_kernel(
         for q in range(4):
             nc.sync.dma_start(out=es_p[32 * q : 32 * q + 4, :].bitcast(I32), in_=es_g[E_ROW + 4 * q : E_ROW + 4 * q + 4, :].bitcast(I32))
         ha_g = keep.tile([P, U], F32, align_bytes=64)
-        nc.vector.tensor_copy(ha_g[:, 0 : U // 2], ha_win[:].indirect(sv_t[:, 0 : U // 32]))
+        nc.vector.tensor_copy(ha_g[:], ha_win[:].indirect(sv_t[:]))
         nc.vector.tensor_copy(xs_g[:], xs_win[:].indirect(offs_t[:]))
         es_members = es_p[:].rearrange("p (v d) -> p d v", d=D)
 
@@ -108,14 +110,22 @@ def tile_picked_yrbf_tanh_p_kernel(
                 out=w_bf[:].rearrange("p t m j -> p m j t")[:, ms],
                 in_=w_raw[:].rearrange("p j (m t) -> p m j t", t=PACK)[:, ms],
             )
-        w_q = keep.tile([P, H], U32, align_bytes=64)
+        own_ps = bank(4)
+        for i in range(TB):
+            nc.tensor.transpose(own_ps[:, i * P : (i + 1) * P], own_col[:, i : i + 1].to_broadcast([P, P]), ident[:])
+        consts = keep.tile([P, S + 2 * D], F32, tag="w1", align_bytes=64)
+        own_row = consts[:, 0:S]
+        nc.scalar.copy(
+            out=own_row.rearrange("p (n i) -> p n i", i=TB), in_=own_ps[:].rearrange("p (i n) -> p n i", i=TB)
+        )
+
+        w_q = keep.tile([P, H], U32, tag="own", align_bytes=64)
         w_s = keep.tile([P, H], U8, align_bytes=64)
         nc.vector.quantize_mx(out=w_q[:].bitcast(FP8X4), scales=w_s[:], in_=w_bf[:].rearrange("p t m j -> p (t m j)"))
 
         xw_g = keep.tile([P, S], U32, align_bytes=64)
         nc.vector.tensor_copy(xw_g[:], xw_win[:].indirect(offs_t[:]))
         es_d = deal_scales(slice(0, FIRST), keep.tile([P, FIRST * V], U8, align_bytes=64, name="es_first"))
-        nc.vector.tensor_copy(ha_g[:, U // 2 : U], ha_win[:].indirect(sv_t[:, U // 32 : U // 16]))
         half_col = keep.tile([P, D], F32, align_bytes=64)
         coef = keep.tile([P, D], F32, align_bytes=64)
         nc.sync.dma_start(out=half_col[:], in_=ha_g[HALF_ROW : HALF_ROW + 1, :])
@@ -152,15 +162,6 @@ def tile_picked_yrbf_tanh_p_kernel(
                     stop=True,
                 )
             nc.scalar.copy(out=h_bf[:, tok, :], in_=h_ps[:].rearrange("p (t n) -> p n t", t=PACK))
-
-        own_ps = bank(4)
-        for i in range(TB):
-            nc.tensor.transpose(own_ps[:, i * P : (i + 1) * P], own_col[:, i : i + 1].to_broadcast([P, P]), ident[:])
-        consts = keep.tile([P, S + 2 * D], F32, tag="w1", align_bytes=64)
-        own_row = consts[:, 0:S]
-        nc.scalar.copy(
-            out=own_row.rearrange("p (n i) -> p n i", i=TB), in_=own_ps[:].rearrange("p (i n) -> p n i", i=TB)
-        )
 
         neg_half = consts[:, S : S + D]
         nc.scalar.activation(neg_half, half_col[:], ACT.Copy, scale=-1.0)

@@ -26,11 +26,6 @@ E_ROW = P - 16
 KEEP_WARM = (4, 5, 6)
 
 
-def load_scale_rows(queue, window, scales):
-    for r in range(4):
-        queue.dma_start(out=window[r:P:32, :].bitcast(I32), in_=scales[0, r:16:4, :].bitcast(I32))
-
-
 def load_words(nc, window, words):
     nc.sync.dma_start(out=window[:].bitcast(I32), in_=words[0].rearrange("p c r -> p (c r)").bitcast(I32))
 
@@ -42,7 +37,8 @@ def tile_picked_yrbf_tanh_p_kernel(
     with ExitStack() as ctx:
         keep = ctx.enter_context(tc.tile_pool(name="keep", bufs=1))
         work = ctx.enter_context(tc.tile_pool(name="work", bufs=14))
-        after_moves = ctx.enter_context(tc.tile_pool(name="after_moves", bufs=1))
+        after_h = ctx.enter_context(tc.tile_pool(name="after_h", bufs=1))
+        after_xs = ctx.enter_context(tc.tile_pool(name="after_xs", bufs=1))
         psum = ctx.enter_context(tc.psum_pool(name="psum", bufs=1))
 
         def bank(b):
@@ -50,19 +46,21 @@ def tile_picked_yrbf_tanh_p_kernel(
 
         offs_t = keep.tile([P, S // 16], U16)
         sv_t = keep.tile([P, U // 16], U16)
-        xs_win = keep.tile([P, T], U8, align_bytes=64)
+        xs_win = after_xs.tile([P, T], U8, align_bytes=64, offset=0)
         es_win = keep.tile([P, W], U8, align_bytes=64)
         ha_win = keep.tile([P, W], F32, align_bytes=64)
         zero = keep.tile([P, 8], F32, align_bytes=64)
 
         diag = keep.tile([P, P], F32)
         ident = keep.tile([P, P], F32)
+        xs_p = keep.tile([P, S], U8, align_bytes=64)
         es_p = keep.tile([P, U], U8, align_bytes=64)
         nc.gpsimd.iota(diag[:], [[1, P]], base=0, channel_multiplier=-1, allow_small_or_imprecise_dtypes=True)
+        nc.vector.memset(es_win[:].bitcast(I32), 0)
         nc.vector.memset(zero[:], 0.0)
-        nc.vector.memset(xs_win[:].bitcast(I32), 0)
-        nc.vector.memset(es_win[0:E_ROW, :].bitcast(I32), 0)
+        nc.vector.memset(xs_win[0:E_ROW, :].bitcast(I32), 0)
         zero_rows = zero[0:HALF_ROW, 0:1].to_broadcast([HALF_ROW, W // 2])
+        nc.vector.memset(xs_p[:].bitcast(I32), 0)
         nc.vector.tensor_copy(ha_win[0:HALF_ROW, 0 : W // 2], zero_rows)
         nc.scalar.copy(ha_win[0:HALF_ROW, W // 2 : W], zero_rows)
         nc.vector.memset(es_p[:].bitcast(I32), 0)
@@ -70,38 +68,46 @@ def tile_picked_yrbf_tanh_p_kernel(
         nc.scalar.activation(diag_sq[:], diag[:], ACT.Square)
         nc.scalar.activation(ident[:], diag_sq[:], ACT.Relu, bias=1.0, scale=-1.0)
 
-        nc.sync.dma_start(out=es_win[E_ROW:P, :].bitcast(I32), in_=e_scales[0].bitcast(I32))
+        nc.sync.dma_start(out=xs_win[E_ROW:P, :].bitcast(I32), in_=x_scales[0].bitcast(I32))
+        nc.sync.dma_start(offs_t[:], offs)
         nc.sync.dma_start(sv_t[:], sv)
         nc.sync.dma_start(out=ha_win[HALF_ROW : HALF_ROW + 1, :], in_=half[0:1, :])
         nc.sync.dma_start(out=ha_win[ALPHA_ROW : ALPHA_ROW + 1, :], in_=alpha[0:1, :])
-        nc.sync.dma_start(offs_t[:], offs)
+        nc.sync.dma_start(out=es_win[0:P:8, :].bitcast(I32), in_=e_scales[0].bitcast(I32))
         w_raw = keep.tile([P, PACK, H], F32, tag="w1", align_bytes=64)
-        w_rows = w1.rearrange("(p j) c -> p j c", j=PACK)
-        for g in range(2):
-            cols = slice(g * (H // 2), (g + 1) * (H // 2))
-            nc.sync.dma_start(out=w_raw[:, :, cols], in_=w_rows[:, :, cols])
-        load_scale_rows(nc.sync, xs_win, x_scales)
-        own_col = keep.tile([P, TB], F32, tag="own", align_bytes=64)
-        nc.sync.dma_start(out=own_col[:], in_=own.rearrange("(p i) o -> p (i o)", i=TB))
-        xw_win = keep.tile([P, T], U32, tag="x_table", align_bytes=64)
+        nc.sync.dma_start(out=w_raw[:], in_=w1.rearrange("(p j) c -> p j c", j=PACK))
+        xw_win = keep.tile([P, T], U32, align_bytes=64)
         load_words(nc, xw_win, x_words)
-        ew_win = keep.tile([P, W], U32, align_bytes=64, tag="e_table")
-        load_words(nc, ew_win, e_words)
 
-        es_g = after_moves.tile([P, U], U8, align_bytes=64, offset=4 * S)
         xs_g = keep.tile([P, S], U8, align_bytes=64)
-
-        nc.vector.tensor_copy(es_g[:], es_win[:].indirect(sv_t[:]))
+        nc.vector.tensor_copy(xs_g[:], xs_win[:].indirect(offs_t[:]))
         for q in range(4):
-            nc.sync.dma_start(out=es_p[32 * q : 32 * q + 4, :].bitcast(I32), in_=es_g[E_ROW + 4 * q : E_ROW + 4 * q + 4, :].bitcast(I32))
+            nc.sync.dma_start(
+                out=xs_p[32 * q : 32 * q + 4, :].bitcast(I32), in_=xs_g[E_ROW + 4 * q : E_ROW + 4 * q + 4, :].bitcast(I32)
+            )
+        ew_win = after_xs.tile([P, W], U32, align_bytes=64, offset=64)
+        load_words(nc, ew_win, e_words)
+        own_col = after_xs.tile([P, TB], F32, align_bytes=64, offset=0)
+        nc.sync.dma_start(out=own_col[:], in_=own.rearrange("(p i) o -> p (i o)", i=TB))
+
+        es_g = keep.tile([P, U], U8, align_bytes=64, tag="e_scales")
+        nc.vector.tensor_copy(es_g[:], es_win[:].indirect(sv_t[:]))
+        for hi in range(2):
+            for q in range(4):
+                nc.sync.dma_start(
+                    out=es_p[32 * q + 4 * hi : 32 * q + 4 * hi + 4, 0 : U - 4 * hi].bitcast(I32),
+                    in_=es_g[32 * q : 32 * q + 32 : 8, 4 * hi : U].bitcast(I32),
+                )
         ha_g = keep.tile([P, U], F32, align_bytes=64)
         nc.vector.tensor_copy(ha_g[:], ha_win[:].indirect(sv_t[:]))
-        nc.vector.tensor_copy(xs_g[:], xs_win[:].indirect(offs_t[:]))
         es_members = es_p[:].rearrange("p (v d) -> p d v", d=D)
 
         def deal_scales(members, dealt):
             nc.vector.tensor_copy(out=dealt[:].rearrange("p (d v) -> p d v", v=V), in_=es_members[:, members, :])
             return [dealt[:, d * V : (d + 1) * V] for d in range(members.stop - members.start)]
+
+        def scale_plane(d):
+            return es_d[d % 4][4 * (d // 4) : P, :]
 
         w_bf = keep.tile([P, PACK, P, PACK], BF16, align_bytes=64)
         for g in range(2):
@@ -110,16 +116,7 @@ def tile_picked_yrbf_tanh_p_kernel(
                 out=w_bf[:].rearrange("p t m j -> p m j t")[:, ms],
                 in_=w_raw[:].rearrange("p j (m t) -> p m j t", t=PACK)[:, ms],
             )
-        own_ps = bank(4)
-        for i in range(TB):
-            nc.tensor.transpose(own_ps[:, i * P : (i + 1) * P], own_col[:, i : i + 1].to_broadcast([P, P]), ident[:])
-        consts = keep.tile([P, S + 2 * D], F32, tag="w1", align_bytes=64)
-        own_row = consts[:, 0:S]
-        nc.scalar.copy(
-            out=own_row.rearrange("p (n i) -> p n i", i=TB), in_=own_ps[:].rearrange("p (i n) -> p n i", i=TB)
-        )
-
-        w_q = keep.tile([P, H], U32, tag="own", align_bytes=64)
+        w_q = keep.tile([P, H], U32, align_bytes=64)
         w_s = keep.tile([P, H], U8, align_bytes=64)
         nc.vector.quantize_mx(out=w_q[:].bitcast(FP8X4), scales=w_s[:], in_=w_bf[:].rearrange("p t m j -> p (t m j)"))
 
@@ -146,7 +143,11 @@ def tile_picked_yrbf_tanh_p_kernel(
 
         ew_d = deal_words(slice(0, FIRST), keep.tile([P, FIRST * V], U32, align_bytes=64, name="ew_first"), pieces=2)
 
-        h_bf = keep.tile([P, S, PACK], BF16, align_bytes=64, tag="h_bf")
+        halves = [slice(0, S // 2), slice(S // 2, S)]
+        h_bf = [
+            after_h.tile([P, S // 2, PACK], BF16, align_bytes=64, name="h_low", offset=0),
+            keep.tile([P, S // 2, PACK], BF16, align_bytes=64, name="h_high"),
+        ]
         for i in range(TB):
             tok = slice(i * P, (i + 1) * P)
             h_ps = bank(i)
@@ -157,30 +158,38 @@ def tile_picked_yrbf_tanh_p_kernel(
                     lhsT=w_q[:, col].bitcast(FP8X4),
                     lhsT_scale=w_s[:, col],
                     rhs=xw_g[:, tok].bitcast(FP8X4),
-                    rhs_scale=xs_g[:, tok],
+                    rhs_scale=xs_p[:, tok],
                     start=True,
                     stop=True,
                 )
-            nc.scalar.copy(out=h_bf[:, tok, :], in_=h_ps[:].rearrange("p (t n) -> p n t", t=PACK))
+            nc.scalar.copy(out=h_bf[i // 2][:, (i % 2) * P : (i % 2 + 1) * P, :], in_=h_ps[:].rearrange("p (t n) -> p n t", t=PACK))
+
+        own_ps = bank(7)
+        for i in range(TB):
+            nc.tensor.transpose(own_ps[:, i * P : (i + 1) * P], own_col[:, i : i + 1].to_broadcast([P, P]), ident[:])
+        consts = keep.tile([P, S + 2 * D], F32, tag="w1", align_bytes=64)
+        own_row = consts[:, 0:S]
+        nc.scalar.copy(
+            out=own_row.rearrange("p (n i) -> p n i", i=TB), in_=own_ps[:].rearrange("p (i n) -> p n i", i=TB)
+        )
 
         neg_half = consts[:, S : S + D]
         nc.scalar.activation(neg_half, half_col[:], ACT.Copy, scale=-1.0)
 
-        h_q = after_moves.tile([P, S], U32, align_bytes=64, offset=64)
+        h_q = keep.tile([P, S], U32, align_bytes=64, tag="e_scales")
         h_s = keep.tile([P, S], U8, align_bytes=64)
-        halves = [slice(0, S // 2), slice(S // 2, S)]
-        for c in halves:
-            nc.vector.quantize_mx(out=h_q[:, c].bitcast(FP8X4), scales=h_s[:, c], in_=h_bf[:, c, :].rearrange("p n t -> p (n t)"))
-        ew_d.extend(deal_words(slice(FIRST, 4), after_moves.tile([P, (4 - FIRST) * V], U32, align_bytes=64, name="ew_second", offset=4 * S + 64 + (D - FIRST) * V)))
-        es_d.extend(deal_scales(slice(FIRST, D), after_moves.tile([P, (D - FIRST) * V], U8, align_bytes=64, name="es_rest", offset=4 * S + 64)))
-        ew_d.extend(deal_words(slice(4, D), keep.tile([P, 4 * V], U32, align_bytes=64, name="ew_high", tag="h_bf")))
+        for c, h_half in zip(halves, h_bf):
+            nc.vector.quantize_mx(out=h_q[:, c].bitcast(FP8X4), scales=h_s[:, c], in_=h_half[:].rearrange("p n t -> p (n t)"))
+        ew_d.extend(deal_words(slice(FIRST, 4), after_h.tile([P, (4 - FIRST) * V], U32, align_bytes=64, name="ew_second", offset=0)))
+        es_d.extend(deal_scales(slice(FIRST, 4), after_h.tile([P, (4 - FIRST) * V], U8, align_bytes=64, name="es_rest", offset=1024)))
+        ew_d.extend(deal_words(slice(4, D), after_h.tile([P, 4 * V], U32, align_bytes=64, name="ew_high", offset=1536)))
 
         def second_product(d, c, b):
             y_ps = bank(b)
             nc.tensor.matmul_mx(
                 out=y_ps[:, c],
                 lhsT=ew_d[d].bitcast(FP8X4),
-                lhsT_scale=es_d[d],
+                lhsT_scale=scale_plane(d),
                 rhs=h_q[:, c].bitcast(FP8X4),
                 rhs_scale=h_s[:, c],
                 start=True,

@@ -19,10 +19,11 @@ FP8X4 = mybir.dt.float8_e4m3fn_x4
 ALU = mybir.AluOpType
 ACT = mybir.ActivationFunctionType
 
-HALF_ROW, ALPHA_ROW = P - 2, P - 1
+HALF_ROW, ALPHA_ROW = 0, 64
 GP_TILES = 4
 FIRST = 2
-E_ROW = P - 16
+X_ROW = P - 16
+E_ROW = 48
 KEEP_WARM = (4, 5, 6)
 
 
@@ -39,6 +40,7 @@ def tile_picked_yrbf_tanh_p_kernel(
         work = ctx.enter_context(tc.tile_pool(name="work", bufs=14))
         after_h = ctx.enter_context(tc.tile_pool(name="after_h", bufs=1))
         after_xs = ctx.enter_context(tc.tile_pool(name="after_xs", bufs=1))
+        after_w = ctx.enter_context(tc.tile_pool(name="after_w", bufs=1))
         psum = ctx.enter_context(tc.psum_pool(name="psum", bufs=1))
 
         def bank(b):
@@ -56,34 +58,33 @@ def tile_picked_yrbf_tanh_p_kernel(
         xs_p = keep.tile([P, S], U8, align_bytes=64)
         es_p = keep.tile([P, U], U8, align_bytes=64)
         nc.gpsimd.iota(diag[:], [[1, P]], base=0, channel_multiplier=-1, allow_small_or_imprecise_dtypes=True)
-        nc.vector.memset(es_win[:].bitcast(I32), 0)
         nc.vector.memset(zero[:], 0.0)
-        nc.vector.memset(xs_win[0:E_ROW, :].bitcast(I32), 0)
-        zero_rows = zero[0:HALF_ROW, 0:1].to_broadcast([HALF_ROW, W // 2])
+        nc.vector.memset(xs_win[0:X_ROW, :].bitcast(I32), 0)
+        nc.vector.memset(es_win[0:E_ROW, :].bitcast(I32), 0)
+        nc.vector.memset(es_win[E_ROW + 16 : P, :].bitcast(I32), 0)
         nc.vector.memset(xs_p[:].bitcast(I32), 0)
-        nc.vector.tensor_copy(ha_win[0:HALF_ROW, 0 : W // 2], zero_rows)
-        nc.scalar.copy(ha_win[0:HALF_ROW, W // 2 : W], zero_rows)
+        nc.scalar.copy(ha_win[:], zero[:, 0:1].to_broadcast([P, W]))
         nc.vector.memset(es_p[:].bitcast(I32), 0)
         diag_sq = keep.tile([P, P], F32)
         nc.scalar.activation(diag_sq[:], diag[:], ACT.Square)
         nc.scalar.activation(ident[:], diag_sq[:], ACT.Relu, bias=1.0, scale=-1.0)
 
-        nc.sync.dma_start(out=xs_win[E_ROW:P, :].bitcast(I32), in_=x_scales[0].bitcast(I32))
+        nc.sync.dma_start(out=xs_win[X_ROW:P, :].bitcast(I32), in_=x_scales[0].bitcast(I32))
         nc.sync.dma_start(offs_t[:], offs)
         nc.sync.dma_start(sv_t[:], sv)
-        nc.sync.dma_start(out=ha_win[HALF_ROW : HALF_ROW + 1, :], in_=half[0:1, :])
-        nc.sync.dma_start(out=ha_win[ALPHA_ROW : ALPHA_ROW + 1, :], in_=alpha[0:1, :])
-        nc.sync.dma_start(out=es_win[0:P:8, :].bitcast(I32), in_=e_scales[0].bitcast(I32))
-        w_raw = keep.tile([P, PACK, H], F32, tag="w1", align_bytes=64)
+        nc.sync.dma_start(out=es_win[E_ROW : E_ROW + 16, :].bitcast(I32), in_=e_scales[0].bitcast(I32))
+        w_raw = after_w.tile([P, PACK, H], F32, align_bytes=64, offset=0)
         nc.sync.dma_start(out=w_raw[:], in_=w1.rearrange("(p j) c -> p j c", j=PACK))
         xw_win = keep.tile([P, T], U32, align_bytes=64)
         load_words(nc, xw_win, x_words)
+        nc.sync.dma_start(out=ha_win[HALF_ROW : HALF_ROW + 1, :], in_=half[0:1, :])
+        nc.sync.dma_start(out=ha_win[ALPHA_ROW : ALPHA_ROW + 1, :], in_=alpha[0:1, :])
 
         xs_g = keep.tile([P, S], U8, align_bytes=64)
         nc.vector.tensor_copy(xs_g[:], xs_win[:].indirect(offs_t[:]))
         for q in range(4):
             nc.sync.dma_start(
-                out=xs_p[32 * q : 32 * q + 4, :].bitcast(I32), in_=xs_g[E_ROW + 4 * q : E_ROW + 4 * q + 4, :].bitcast(I32)
+                out=xs_p[32 * q : 32 * q + 4, :].bitcast(I32), in_=xs_g[X_ROW + 4 * q : X_ROW + 4 * q + 4, :].bitcast(I32)
             )
         ew_win = after_xs.tile([P, W], U32, align_bytes=64, offset=64)
         load_words(nc, ew_win, e_words)
@@ -96,10 +97,8 @@ def tile_picked_yrbf_tanh_p_kernel(
             for q in range(4):
                 nc.sync.dma_start(
                     out=es_p[32 * q + 4 * hi : 32 * q + 4 * hi + 4, 0 : U - 4 * hi].bitcast(I32),
-                    in_=es_g[32 * q : 32 * q + 32 : 8, 4 * hi : U].bitcast(I32),
+                    in_=es_g[E_ROW + 4 * q : E_ROW + 4 * q + 4, 4 * hi : U].bitcast(I32),
                 )
-        ha_g = keep.tile([P, U], F32, align_bytes=64)
-        nc.vector.tensor_copy(ha_g[:], ha_win[:].indirect(sv_t[:]))
         es_members = es_p[:].rearrange("p (v d) -> p d v", d=D)
 
         def deal_scales(members, dealt):
@@ -116,12 +115,15 @@ def tile_picked_yrbf_tanh_p_kernel(
                 out=w_bf[:].rearrange("p t m j -> p m j t")[:, ms],
                 in_=w_raw[:].rearrange("p j (m t) -> p m j t", t=PACK)[:, ms],
             )
+        ha_g = after_w.tile([P, U], F32, align_bytes=64, offset=0)
+        nc.scalar.activation(ha_g[:], ha_win[:].indirect(sv_t[:]), ACT.Copy)
         w_q = keep.tile([P, H], U32, align_bytes=64)
         w_s = keep.tile([P, H], U8, align_bytes=64)
         nc.vector.quantize_mx(out=w_q[:].bitcast(FP8X4), scales=w_s[:], in_=w_bf[:].rearrange("p t m j -> p (t m j)"))
 
         xw_g = keep.tile([P, S], U32, align_bytes=64)
-        nc.vector.tensor_copy(xw_g[:], xw_win[:].indirect(offs_t[:]))
+        for i in range(TB):
+            nc.vector.tensor_copy(xw_g[:, i * P : (i + 1) * P], xw_win[:].indirect(offs_t[:, i * P // 16 : (i + 1) * P // 16]))
         es_d = deal_scales(slice(0, FIRST), keep.tile([P, FIRST * V], U8, align_bytes=64, name="es_first"))
         half_col = keep.tile([P, D], F32, align_bytes=64)
         coef = keep.tile([P, D], F32, align_bytes=64)
@@ -167,7 +169,7 @@ def tile_picked_yrbf_tanh_p_kernel(
         own_ps = bank(7)
         for i in range(TB):
             nc.tensor.transpose(own_ps[:, i * P : (i + 1) * P], own_col[:, i : i + 1].to_broadcast([P, P]), ident[:])
-        consts = keep.tile([P, S + 2 * D], F32, tag="w1", align_bytes=64)
+        consts = after_w.tile([P, S + 2 * D], F32, align_bytes=64, offset=4096)
         own_row = consts[:, 0:S]
         nc.scalar.copy(
             out=own_row.rearrange("p (n i) -> p n i", i=TB), in_=own_ps[:].rearrange("p (i n) -> p n i", i=TB)

@@ -63,7 +63,7 @@ def tile_picked_yrbf_tanh_p_kernel(
         nc.vector.memset(es_win[0:E_ROW, :].bitcast(I32), 0)
         nc.vector.memset(es_win[E_ROW + 16 : P, :].bitcast(I32), 0)
         nc.vector.memset(xs_p[:].bitcast(I32), 0)
-        nc.scalar.copy(ha_win[:], zero[:, 0:1].to_broadcast([P, W]))
+        nc.scalar.activation(ha_win[:], zero[:, 0:1].to_broadcast([P, W]), ACT.Copy)
         nc.vector.memset(es_p[:].bitcast(I32), 0)
         diag_sq = keep.tile([P, P], F32)
         nc.scalar.activation(diag_sq[:], diag[:], ACT.Square)
@@ -93,12 +93,10 @@ def tile_picked_yrbf_tanh_p_kernel(
 
         es_g = keep.tile([P, U], U8, align_bytes=64, tag="e_scales")
         nc.vector.tensor_copy(es_g[:], es_win[:].indirect(sv_t[:]))
-        for hi in range(2):
-            for q in range(4):
-                nc.sync.dma_start(
-                    out=es_p[32 * q + 4 * hi : 32 * q + 4 * hi + 4, 0 : U - 4 * hi].bitcast(I32),
-                    in_=es_g[E_ROW + 4 * q : E_ROW + 4 * q + 4, 4 * hi : U].bitcast(I32),
-                )
+        for q in range(4):
+            nc.sync.dma_start(
+                out=es_p[32 * q : 32 * q + 4, :].bitcast(I32), in_=es_g[E_ROW + 4 * q : E_ROW + 4 * q + 4, :].bitcast(I32)
+            )
         es_members = es_p[:].rearrange("p (v d) -> p d v", d=D)
 
         def deal_scales(members, dealt):
@@ -106,17 +104,17 @@ def tile_picked_yrbf_tanh_p_kernel(
             return [dealt[:, d * V : (d + 1) * V] for d in range(members.stop - members.start)]
 
         def scale_plane(d):
-            return es_d[d % 4][4 * (d // 4) : P, :]
+            return es_d[d]
 
         w_bf = keep.tile([P, PACK, P, PACK], BF16, align_bytes=64)
         for g in range(2):
             ms = slice(g * (P // 2), (g + 1) * (P // 2))
-            nc.scalar.copy(
+            [nc.scalar.copy, nc.vector.tensor_copy][g](
                 out=w_bf[:].rearrange("p t m j -> p m j t")[:, ms],
                 in_=w_raw[:].rearrange("p j (m t) -> p m j t", t=PACK)[:, ms],
             )
         ha_g = after_w.tile([P, U], F32, align_bytes=64, offset=0)
-        nc.scalar.activation(ha_g[:], ha_win[:].indirect(sv_t[:]), ACT.Copy)
+        nc.scalar.activation(ha_g[:], ha_win[:].indirect(sv_t[:]), ACT.Copy, scale=-1.0)
         w_q = keep.tile([P, H], U32, align_bytes=64)
         w_s = keep.tile([P, H], U8, align_bytes=64)
         nc.vector.quantize_mx(out=w_q[:].bitcast(FP8X4), scales=w_s[:], in_=w_bf[:].rearrange("p t m j -> p (t m j)"))
@@ -125,9 +123,9 @@ def tile_picked_yrbf_tanh_p_kernel(
         for i in range(TB):
             nc.vector.tensor_copy(xw_g[:, i * P : (i + 1) * P], xw_win[:].indirect(offs_t[:, i * P // 16 : (i + 1) * P // 16]))
         es_d = deal_scales(slice(0, FIRST), keep.tile([P, FIRST * V], U8, align_bytes=64, name="es_first"))
-        half_col = keep.tile([P, D], F32, align_bytes=64)
+        neg_half = keep.tile([P, D], F32, align_bytes=64)
         coef = keep.tile([P, D], F32, align_bytes=64)
-        nc.sync.dma_start(out=half_col[:], in_=ha_g[HALF_ROW : HALF_ROW + 1, :])
+        nc.sync.dma_start(out=neg_half[:], in_=ha_g[HALF_ROW : HALF_ROW + 1, :])
         nc.sync.dma_start(out=coef[:], in_=ha_g[ALPHA_ROW : ALPHA_ROW + 1, :])
         ew_g = keep.tile([P, U], U32, align_bytes=64)
         for g in range(2):
@@ -175,16 +173,13 @@ def tile_picked_yrbf_tanh_p_kernel(
             out=own_row.rearrange("p (n i) -> p n i", i=TB), in_=own_ps[:].rearrange("p (i n) -> p n i", i=TB)
         )
 
-        neg_half = consts[:, S : S + D]
-        nc.scalar.activation(neg_half, half_col[:], ACT.Copy, scale=-1.0)
-
         h_q = keep.tile([P, S], U32, align_bytes=64, tag="e_scales")
         h_s = keep.tile([P, S], U8, align_bytes=64)
         for c, h_half in zip(halves, h_bf):
             nc.vector.quantize_mx(out=h_q[:, c].bitcast(FP8X4), scales=h_s[:, c], in_=h_half[:].rearrange("p n t -> p (n t)"))
         ew_d.extend(deal_words(slice(FIRST, 4), after_h.tile([P, (4 - FIRST) * V], U32, align_bytes=64, name="ew_second", offset=0)))
-        es_d.extend(deal_scales(slice(FIRST, 4), after_h.tile([P, (4 - FIRST) * V], U8, align_bytes=64, name="es_rest", offset=1024)))
-        ew_d.extend(deal_words(slice(4, D), after_h.tile([P, 4 * V], U32, align_bytes=64, name="ew_high", offset=1536)))
+        es_d.extend(deal_scales(slice(FIRST, D), after_h.tile([P, (D - FIRST) * V], U8, align_bytes=64, name="es_rest", offset=1024)))
+        ew_d.extend(deal_words(slice(4, D), after_h.tile([P, 4 * V], U32, align_bytes=64, name="ew_high", offset=1792)))
 
         def second_product(d, c, b):
             y_ps = bank(b)
@@ -240,5 +235,5 @@ def tile_picked_yrbf_tanh_p_kernel(
                 weigh_and_add(nc.vector, d, ee[d], blocks)
             for i in blocks:
                 weigh_and_add(nc.vector, D - 1, ee[D - 1], [i])
-                nc.scalar.activation(res[:, i, :], z_ps[i][:, 0:V], ACT.Tanh)
+                nc.scalar.activation(res[:, i, :], z_ps[i][:, 0:V], ACT.Tanh, scale=-1.0)
                 nc.sync.dma_start(out=out_v[:, i, :], in_=res[:, i, :])

@@ -40,6 +40,7 @@ def tile_picked_yrbf_tanh_p_kernel(
         work = ctx.enter_context(tc.tile_pool(name="work", bufs=14))
         after_h = ctx.enter_context(tc.tile_pool(name="after_h", bufs=1))
         after_xs = ctx.enter_context(tc.tile_pool(name="after_xs", bufs=1))
+        after_xw = ctx.enter_context(tc.tile_pool(name="after_xw", bufs=1))
         after_w = ctx.enter_context(tc.tile_pool(name="after_w", bufs=1))
         psum = ctx.enter_context(tc.psum_pool(name="psum", bufs=1))
 
@@ -69,13 +70,13 @@ def tile_picked_yrbf_tanh_p_kernel(
         nc.scalar.activation(diag_sq[:], diag[:], ACT.Square)
         nc.scalar.activation(ident[:], diag_sq[:], ACT.Relu, bias=1.0, scale=-1.0)
 
-        nc.sync.dma_start(out=xs_win[X_ROW:P, :].bitcast(I32), in_=x_scales[0].bitcast(I32))
         nc.sync.dma_start(offs_t[:], offs)
+        nc.sync.dma_start(out=xs_win[X_ROW:P, :].bitcast(I32), in_=x_scales[0].bitcast(I32))
         nc.sync.dma_start(sv_t[:], sv)
         nc.sync.dma_start(out=es_win[E_ROW : E_ROW + 16, :].bitcast(I32), in_=e_scales[0].bitcast(I32))
         w_raw = after_w.tile([P, PACK, H], F32, align_bytes=64, offset=0)
         nc.sync.dma_start(out=w_raw[:], in_=w1.rearrange("(p j) c -> p j c", j=PACK))
-        xw_win = keep.tile([P, T], U32, align_bytes=64)
+        xw_win = after_xw.tile([P, T], U32, align_bytes=64, offset=0)
         load_words(nc, xw_win, x_words)
         nc.sync.dma_start(out=ha_win[HALF_ROW : HALF_ROW + 1, :], in_=half[0:1, :])
         nc.sync.dma_start(out=ha_win[ALPHA_ROW : ALPHA_ROW + 1, :], in_=alpha[0:1, :])
@@ -91,20 +92,8 @@ def tile_picked_yrbf_tanh_p_kernel(
         own_col = after_xs.tile([P, TB], F32, align_bytes=64, offset=0)
         nc.sync.dma_start(out=own_col[:], in_=own.rearrange("(p i) o -> p (i o)", i=TB))
 
-        es_g = keep.tile([P, U], U8, align_bytes=64, tag="e_scales")
+        es_g = keep.tile([P, U], U8, align_bytes=64)
         nc.vector.tensor_copy(es_g[:], es_win[:].indirect(sv_t[:]))
-        for q in range(4):
-            nc.sync.dma_start(
-                out=es_p[32 * q : 32 * q + 4, :].bitcast(I32), in_=es_g[E_ROW + 4 * q : E_ROW + 4 * q + 4, :].bitcast(I32)
-            )
-        es_members = es_p[:].rearrange("p (v d) -> p d v", d=D)
-
-        def deal_scales(members, dealt):
-            nc.vector.tensor_copy(out=dealt[:].rearrange("p (d v) -> p d v", v=V), in_=es_members[:, members, :])
-            return [dealt[:, d * V : (d + 1) * V] for d in range(members.stop - members.start)]
-
-        def scale_plane(d):
-            return es_d[d]
 
         w_bf = keep.tile([P, PACK, P, PACK], BF16, align_bytes=64)
         for g in range(2):
@@ -122,7 +111,12 @@ def tile_picked_yrbf_tanh_p_kernel(
         xw_g = keep.tile([P, S], U32, align_bytes=64)
         for i in range(TB):
             nc.vector.tensor_copy(xw_g[:, i * P : (i + 1) * P], xw_win[:].indirect(offs_t[:, i * P // 16 : (i + 1) * P // 16]))
-        es_d = deal_scales(slice(0, FIRST), keep.tile([P, FIRST * V], U8, align_bytes=64, name="es_first"))
+        es_dealt = after_xw.tile([P, U], U8, align_bytes=64, offset=0)
+        nc.vector.tensor_copy(out=es_dealt[:].rearrange("p (d v) -> p d v", v=V), in_=es_g[:].rearrange("p (v d) -> p d v", d=D))
+        for q in range(4):
+            nc.sync.dma_start(
+                out=es_p[32 * q : 32 * q + 4, :].bitcast(I32), in_=es_dealt[E_ROW + 4 * q : E_ROW + 4 * q + 4, :].bitcast(I32)
+            )
         neg_half = keep.tile([P, D], F32, align_bytes=64)
         coef = keep.tile([P, D], F32, align_bytes=64)
         nc.sync.dma_start(out=neg_half[:], in_=ha_g[HALF_ROW : HALF_ROW + 1, :])
@@ -173,20 +167,19 @@ def tile_picked_yrbf_tanh_p_kernel(
             out=own_row.rearrange("p (n i) -> p n i", i=TB), in_=own_ps[:].rearrange("p (i n) -> p n i", i=TB)
         )
 
-        h_q = keep.tile([P, S], U32, align_bytes=64, tag="e_scales")
+        h_q = after_xw.tile([P, S], U32, align_bytes=64, offset=0)
         h_s = keep.tile([P, S], U8, align_bytes=64)
         for c, h_half in zip(halves, h_bf):
             nc.vector.quantize_mx(out=h_q[:, c].bitcast(FP8X4), scales=h_s[:, c], in_=h_half[:].rearrange("p n t -> p (n t)"))
         ew_d.extend(deal_words(slice(FIRST, 4), after_h.tile([P, (4 - FIRST) * V], U32, align_bytes=64, name="ew_second", offset=0)))
-        es_d.extend(deal_scales(slice(FIRST, D), after_h.tile([P, (D - FIRST) * V], U8, align_bytes=64, name="es_rest", offset=1024)))
-        ew_d.extend(deal_words(slice(4, D), after_h.tile([P, 4 * V], U32, align_bytes=64, name="ew_high", offset=1792)))
+        ew_d.extend(deal_words(slice(4, D), after_h.tile([P, 4 * V], U32, align_bytes=64, name="ew_high", offset=1024)))
 
         def second_product(d, c, b):
             y_ps = bank(b)
             nc.tensor.matmul_mx(
                 out=y_ps[:, c],
                 lhsT=ew_d[d].bitcast(FP8X4),
-                lhsT_scale=scale_plane(d),
+                lhsT_scale=es_p[:, d * V : (d + 1) * V],
                 rhs=h_q[:, c].bitcast(FP8X4),
                 rhs_scale=h_s[:, c],
                 start=True,

@@ -19,12 +19,11 @@ FP8X4 = mybir.dt.float8_e4m3fn_x4
 ALU = mybir.AluOpType
 ACT = mybir.ActivationFunctionType
 
-HALF_ROW, ALPHA_ROW = 0, 64
-GP_TILES = 4
+HALF_ROW, ALPHA_ROW = P - 2, P - 1
+GP_TILES = 5
 FIRST = 2
 X_ROW = P - 16
 E_ROW = 48
-KEEP_WARM = (4, 5, 6)
 
 
 def load_words(nc, window, words):
@@ -64,7 +63,7 @@ def tile_picked_yrbf_tanh_p_kernel(
         nc.vector.memset(es_win[0:E_ROW, :].bitcast(I32), 0)
         nc.vector.memset(es_win[E_ROW + 16 : P, :].bitcast(I32), 0)
         nc.vector.memset(xs_p[:].bitcast(I32), 0)
-        nc.scalar.activation(ha_win[:], zero[:, 0:1].to_broadcast([P, W]), ACT.Copy)
+        nc.scalar.activation(ha_win[0:HALF_ROW, :], zero[0:HALF_ROW, 0:1].to_broadcast([HALF_ROW, W]), ACT.Copy)
         nc.vector.memset(es_p[:].bitcast(I32), 0)
         diag_sq = keep.tile([P, P], F32)
         nc.scalar.activation(diag_sq[:], diag[:], ACT.Square)
@@ -76,10 +75,10 @@ def tile_picked_yrbf_tanh_p_kernel(
         nc.sync.dma_start(out=es_win[E_ROW : E_ROW + 16, :].bitcast(I32), in_=e_scales[0].bitcast(I32))
         w_raw = after_w.tile([P, PACK, H], F32, align_bytes=64, offset=0)
         nc.sync.dma_start(out=w_raw[:], in_=w1.rearrange("(p j) c -> p j c", j=PACK))
-        xw_win = after_xw.tile([P, T], U32, align_bytes=64, offset=0)
+        xw_win = keep.tile([P, T], U32, align_bytes=64)
         load_words(nc, xw_win, x_words)
-        nc.sync.dma_start(out=ha_win[HALF_ROW : HALF_ROW + 1, :], in_=half[0:1, :])
-        nc.sync.dma_start(out=ha_win[ALPHA_ROW : ALPHA_ROW + 1, :], in_=alpha[0:1, :])
+        nc.scalar.dma_start(out=ha_win[HALF_ROW : HALF_ROW + 1, :], in_=half[0:1, :])
+        nc.scalar.dma_start(out=ha_win[ALPHA_ROW : ALPHA_ROW + 1, :], in_=alpha[0:1, :])
 
         xs_g = keep.tile([P, S], U8, align_bytes=64)
         nc.vector.tensor_copy(xs_g[:], xs_win[:].indirect(offs_t[:]))
@@ -95,7 +94,7 @@ def tile_picked_yrbf_tanh_p_kernel(
         es_g = keep.tile([P, U], U8, align_bytes=64)
         nc.vector.tensor_copy(es_g[:], es_win[:].indirect(sv_t[:]))
 
-        w_bf = keep.tile([P, PACK, P, PACK], BF16, align_bytes=64)
+        w_bf = after_xw.tile([P, PACK, P, PACK], BF16, align_bytes=64, offset=0)
         for g in range(2):
             ms = slice(g * (P // 2), (g + 1) * (P // 2))
             [nc.scalar.copy, nc.vector.tensor_copy][g](
@@ -167,7 +166,7 @@ def tile_picked_yrbf_tanh_p_kernel(
             out=own_row.rearrange("p (n i) -> p n i", i=TB), in_=own_ps[:].rearrange("p (i n) -> p n i", i=TB)
         )
 
-        h_q = after_xw.tile([P, S], U32, align_bytes=64, offset=0)
+        h_q = after_xs.tile([P, S], U32, align_bytes=64, offset=T)
         h_s = keep.tile([P, S], U8, align_bytes=64)
         for c, h_half in zip(halves, h_bf):
             nc.vector.quantize_mx(out=h_q[:, c].bitcast(FP8X4), scales=h_s[:, c], in_=h_half[:].rearrange("p n t -> p (n t)"))
@@ -203,7 +202,7 @@ def tile_picked_yrbf_tanh_p_kernel(
 
         whole = slice(0, S)
         first = [second_product(0, c, b) for c, b in zip(halves, (4, 3))]
-        y_ps = [None] + [second_product(d, whole, (4 + d) % 8) for d in range(1, D - 1)]
+        y_ps = [None] + [second_product(d, whole, (4 + d) % 8) for d in range(1, D - 2)]
         ee = []
         for d in range(D):
             arg = work.tile([P, S], F32)
@@ -212,11 +211,9 @@ def tile_picked_yrbf_tanh_p_kernel(
                 y = first[g] if d == 0 else y_ps[d]
                 nc.vector.scalar_tensor_tensor(arg[:, c], own_row[:, c], 2.0, y[:, c], ALU.mult, ALU.add)
                 nc.scalar.activation(ee[d][:, c], arg[:, c], ACT.Exp, bias=neg_half[:, d : d + 1], scale=0.5)
-            if d == 0:
-                y_ps.append(second_product(D - 1, whole, 3))
-            if d in KEEP_WARM:
-                second_product(d, whole, (4 + d) % 8)
-        z_ps = [bank(4 + i) for i in range(TB)]
+            if d in (3, 4):
+                y_ps.append(second_product(d + 3, whole, (4 + d) % 8))
+        z_ps = [bank(2 + i) for i in range(TB)]
         for d in range(GP_TILES):
             weigh_and_add(nc.gpsimd, d, ee[d], range(TB))
 

@@ -20,10 +20,10 @@ ALU = mybir.AluOpType
 ACT = mybir.ActivationFunctionType
 
 HALF_ROW, ALPHA_ROW = P - 2, P - 1
-GP_TILES = 5
+GP_TILES = 4
 FIRST = 2
-X_ROW = P - 16
-E_ROW = 48
+X_ROW = 48
+E_ROW = P - 16
 
 
 def load_words(nc, window, words):
@@ -39,7 +39,7 @@ def tile_picked_yrbf_tanh_p_kernel(
         work = ctx.enter_context(tc.tile_pool(name="work", bufs=14))
         after_h = ctx.enter_context(tc.tile_pool(name="after_h", bufs=1))
         after_xs = ctx.enter_context(tc.tile_pool(name="after_xs", bufs=1))
-        after_xw = ctx.enter_context(tc.tile_pool(name="after_xw", bufs=1))
+        after_wq = ctx.enter_context(tc.tile_pool(name="after_wq", bufs=1))
         after_w = ctx.enter_context(tc.tile_pool(name="after_w", bufs=1))
         psum = ctx.enter_context(tc.psum_pool(name="psum", bufs=1))
 
@@ -60,8 +60,8 @@ def tile_picked_yrbf_tanh_p_kernel(
         nc.gpsimd.iota(diag[:], [[1, P]], base=0, channel_multiplier=-1, allow_small_or_imprecise_dtypes=True)
         nc.vector.memset(zero[:], 0.0)
         nc.vector.memset(xs_win[0:X_ROW, :].bitcast(I32), 0)
+        nc.vector.memset(xs_win[X_ROW + 16 : P, :].bitcast(I32), 0)
         nc.vector.memset(es_win[0:E_ROW, :].bitcast(I32), 0)
-        nc.vector.memset(es_win[E_ROW + 16 : P, :].bitcast(I32), 0)
         nc.vector.memset(xs_p[:].bitcast(I32), 0)
         nc.scalar.activation(ha_win[0:HALF_ROW, :], zero[0:HALF_ROW, 0:1].to_broadcast([HALF_ROW, W]), ACT.Copy)
         nc.vector.memset(es_p[:].bitcast(I32), 0)
@@ -70,7 +70,7 @@ def tile_picked_yrbf_tanh_p_kernel(
         nc.scalar.activation(ident[:], diag_sq[:], ACT.Relu, bias=1.0, scale=-1.0)
 
         nc.sync.dma_start(offs_t[:], offs)
-        nc.sync.dma_start(out=xs_win[X_ROW:P, :].bitcast(I32), in_=x_scales[0].bitcast(I32))
+        nc.sync.dma_start(out=xs_win[X_ROW : X_ROW + 16, :].bitcast(I32), in_=x_scales[0].bitcast(I32))
         nc.sync.dma_start(sv_t[:], sv)
         nc.sync.dma_start(out=es_win[E_ROW : E_ROW + 16, :].bitcast(I32), in_=e_scales[0].bitcast(I32))
         w_raw = after_w.tile([P, PACK, H], F32, align_bytes=64, offset=0)
@@ -94,7 +94,7 @@ def tile_picked_yrbf_tanh_p_kernel(
         es_g = keep.tile([P, U], U8, align_bytes=64)
         nc.vector.tensor_copy(es_g[:], es_win[:].indirect(sv_t[:]))
 
-        w_bf = after_xw.tile([P, PACK, P, PACK], BF16, align_bytes=64, offset=0)
+        w_bf = after_wq.tile([P, PACK, P, PACK], BF16, align_bytes=64, offset=0)
         for g in range(2):
             ms = slice(g * (P // 2), (g + 1) * (P // 2))
             [nc.scalar.copy, nc.vector.tensor_copy][g](
@@ -107,10 +107,10 @@ def tile_picked_yrbf_tanh_p_kernel(
         w_s = keep.tile([P, H], U8, align_bytes=64)
         nc.vector.quantize_mx(out=w_q[:].bitcast(FP8X4), scales=w_s[:], in_=w_bf[:].rearrange("p t m j -> p (t m j)"))
 
-        xw_g = keep.tile([P, S], U32, align_bytes=64)
+        xw_g = after_wq.tile([P, S], U32, align_bytes=64, offset=0)
         for i in range(TB):
             nc.vector.tensor_copy(xw_g[:, i * P : (i + 1) * P], xw_win[:].indirect(offs_t[:, i * P // 16 : (i + 1) * P // 16]))
-        es_dealt = after_xw.tile([P, U], U8, align_bytes=64, offset=0)
+        es_dealt = after_w.tile([P, U], U8, align_bytes=64, offset=7168)
         nc.vector.tensor_copy(out=es_dealt[:].rearrange("p (d v) -> p d v", v=V), in_=es_g[:].rearrange("p (v d) -> p d v", d=D))
         for q in range(4):
             nc.sync.dma_start(

@@ -19,8 +19,9 @@ FP8X4 = mybir.dt.float8_e4m3fn_x4
 ALU = mybir.AluOpType
 ACT = mybir.ActivationFunctionType
 
-HALF_ROW, ALPHA_ROW = P - 2, P - 1
+HALF_ROW, ALPHA_ROW = 4, 8
 GP_TILES = 4
+CLEAR_SHARE = 1408
 FIRST = 2
 X_ROW = 48
 E_ROW = P - 16
@@ -41,6 +42,7 @@ def tile_picked_yrbf_tanh_p_kernel(
         after_xs = ctx.enter_context(tc.tile_pool(name="after_xs", bufs=1))
         after_wq = ctx.enter_context(tc.tile_pool(name="after_wq", bufs=1))
         after_w = ctx.enter_context(tc.tile_pool(name="after_w", bufs=1))
+        after_zero = ctx.enter_context(tc.tile_pool(name="after_zero", bufs=1))
         psum = ctx.enter_context(tc.psum_pool(name="psum", bufs=1))
 
         def bank(b):
@@ -51,7 +53,7 @@ def tile_picked_yrbf_tanh_p_kernel(
         xs_win = after_xs.tile([P, T], U8, align_bytes=64, offset=0)
         es_win = keep.tile([P, W], U8, align_bytes=64)
         ha_win = keep.tile([P, W], F32, align_bytes=64)
-        zero = keep.tile([P, 8], F32, align_bytes=64)
+        zero = after_zero.tile([P, 8], F32, align_bytes=64, offset=0)
 
         diag = keep.tile([P, P], F32)
         ident = keep.tile([P, P], F32)
@@ -59,11 +61,12 @@ def tile_picked_yrbf_tanh_p_kernel(
         es_p = keep.tile([P, U], U8, align_bytes=64)
         nc.gpsimd.iota(diag[:], [[1, P]], base=0, channel_multiplier=-1, allow_small_or_imprecise_dtypes=True)
         nc.vector.memset(zero[:], 0.0)
+        nc.vector.memset(ha_win[:, 0:CLEAR_SHARE], 0.0)
         nc.vector.memset(xs_win[0:X_ROW, :].bitcast(I32), 0)
         nc.vector.memset(xs_win[X_ROW + 16 : P, :].bitcast(I32), 0)
         nc.vector.memset(es_win[0:E_ROW, :].bitcast(I32), 0)
         nc.vector.memset(xs_p[:].bitcast(I32), 0)
-        nc.scalar.activation(ha_win[0:HALF_ROW, :], zero[0:HALF_ROW, 0:1].to_broadcast([HALF_ROW, W]), ACT.Copy)
+        nc.scalar.copy(ha_win[:, CLEAR_SHARE:W], zero[:, 0:1].to_broadcast([P, W - CLEAR_SHARE]))
         nc.vector.memset(es_p[:].bitcast(I32), 0)
         diag_sq = keep.tile([P, P], F32)
         nc.scalar.activation(diag_sq[:], diag[:], ACT.Square)
@@ -75,10 +78,10 @@ def tile_picked_yrbf_tanh_p_kernel(
         nc.sync.dma_start(out=es_win[E_ROW : E_ROW + 16, :].bitcast(I32), in_=e_scales[0].bitcast(I32))
         w_raw = after_w.tile([P, PACK, H], F32, align_bytes=64, offset=0)
         nc.sync.dma_start(out=w_raw[:], in_=w1.rearrange("(p j) c -> p j c", j=PACK))
-        xw_win = keep.tile([P, T], U32, align_bytes=64)
+        nc.sync.dma_start(out=ha_win[HALF_ROW : HALF_ROW + 1, :], in_=half[0:1, :])
+        nc.sync.dma_start(out=ha_win[ALPHA_ROW : ALPHA_ROW + 1, :], in_=alpha[0:1, :])
+        xw_win = after_zero.tile([P, T], U32, align_bytes=64, offset=0)
         load_words(nc, xw_win, x_words)
-        nc.scalar.dma_start(out=ha_win[HALF_ROW : HALF_ROW + 1, :], in_=half[0:1, :])
-        nc.scalar.dma_start(out=ha_win[ALPHA_ROW : ALPHA_ROW + 1, :], in_=alpha[0:1, :])
 
         xs_g = keep.tile([P, S], U8, align_bytes=64)
         nc.vector.tensor_copy(xs_g[:], xs_win[:].indirect(offs_t[:]))

@@ -19,10 +19,11 @@ FP8X4 = mybir.dt.float8_e4m3fn_x4
 ALU = mybir.AluOpType
 ACT = mybir.ActivationFunctionType
 
-HALF_ROW, ALPHA_ROW = 4, 8
+HALF_ROW, ALPHA_ROW = 68, 72
 GP_TILES = 4
 CLEAR_SHARE = 1408
 FIRST = 2
+SCALAR_CASTS = 32
 X_ROW = 48
 E_ROW = P - 16
 
@@ -38,7 +39,6 @@ def tile_picked_yrbf_tanh_p_kernel(
     with ExitStack() as ctx:
         keep = ctx.enter_context(tc.tile_pool(name="keep", bufs=1))
         work = ctx.enter_context(tc.tile_pool(name="work", bufs=14))
-        after_h = ctx.enter_context(tc.tile_pool(name="after_h", bufs=1))
         after_xs = ctx.enter_context(tc.tile_pool(name="after_xs", bufs=1))
         after_wq = ctx.enter_context(tc.tile_pool(name="after_wq", bufs=1))
         after_w = ctx.enter_context(tc.tile_pool(name="after_w", bufs=1))
@@ -53,7 +53,7 @@ def tile_picked_yrbf_tanh_p_kernel(
         xs_win = after_xs.tile([P, T], U8, align_bytes=64, offset=0)
         es_win = keep.tile([P, W], U8, align_bytes=64)
         ha_win = keep.tile([P, W], F32, align_bytes=64)
-        zero = after_zero.tile([P, 8], F32, align_bytes=64, offset=0)
+        zero = after_zero.tile([P, 32], F32, align_bytes=64, offset=0)
 
         diag = keep.tile([P, P], F32)
         ident = keep.tile([P, P], F32)
@@ -66,9 +66,11 @@ def tile_picked_yrbf_tanh_p_kernel(
         nc.vector.memset(xs_win[X_ROW + 16 : P, :].bitcast(I32), 0)
         nc.vector.memset(es_win[0:E_ROW, :].bitcast(I32), 0)
         nc.vector.memset(xs_p[:].bitcast(I32), 0)
-        nc.scalar.copy(ha_win[:, CLEAR_SHARE:W], zero[:, 0:1].to_broadcast([P, W - CLEAR_SHARE]))
+        nc.scalar.copy(
+            ha_win[:, CLEAR_SHARE:W].rearrange("p (a b) -> p a b", b=32), zero[:].unsqueeze(1).to_broadcast([P, (W - CLEAR_SHARE) // 32, 32])
+        )
         nc.vector.memset(es_p[:].bitcast(I32), 0)
-        diag_sq = keep.tile([P, P], F32)
+        diag_sq = after_wq.tile([P, P], F32, align_bytes=64, offset=0)
         nc.scalar.activation(diag_sq[:], diag[:], ACT.Square)
         nc.scalar.activation(ident[:], diag_sq[:], ACT.Relu, bias=1.0, scale=-1.0)
 
@@ -80,7 +82,9 @@ def tile_picked_yrbf_tanh_p_kernel(
         nc.sync.dma_start(out=w_raw[:], in_=w1.rearrange("(p j) c -> p j c", j=PACK))
         nc.sync.dma_start(out=ha_win[HALF_ROW : HALF_ROW + 1, :], in_=half[0:1, :])
         nc.sync.dma_start(out=ha_win[ALPHA_ROW : ALPHA_ROW + 1, :], in_=alpha[0:1, :])
-        xw_win = after_zero.tile([P, T], U32, align_bytes=64, offset=0)
+        own_col = after_zero.tile([P, TB], F32, align_bytes=64, offset=0)
+        nc.sync.dma_start(out=own_col[:], in_=own.rearrange("(p i) o -> p (i o)", i=TB))
+        xw_win = after_zero.tile([P, T], U32, align_bytes=64, offset=64)
         load_words(nc, xw_win, x_words)
 
         xs_g = keep.tile([P, S], U8, align_bytes=64)
@@ -91,24 +95,25 @@ def tile_picked_yrbf_tanh_p_kernel(
             )
         ew_win = after_xs.tile([P, W], U32, align_bytes=64, offset=64)
         load_words(nc, ew_win, e_words)
-        own_col = after_xs.tile([P, TB], F32, align_bytes=64, offset=0)
-        nc.sync.dma_start(out=own_col[:], in_=own.rearrange("(p i) o -> p (i o)", i=TB))
 
         es_g = keep.tile([P, U], U8, align_bytes=64)
         nc.vector.tensor_copy(es_g[:], es_win[:].indirect(sv_t[:]))
 
         w_bf = after_wq.tile([P, PACK, P, PACK], BF16, align_bytes=64, offset=0)
-        for g in range(2):
-            ms = slice(g * (P // 2), (g + 1) * (P // 2))
-            [nc.scalar.copy, nc.vector.tensor_copy][g](
-                out=w_bf[:].rearrange("p t m j -> p m j t")[:, ms],
-                in_=w_raw[:].rearrange("p j (m t) -> p m j t", t=PACK)[:, ms],
-            )
+        w_to = w_bf[:].rearrange("p t m j -> p m j t")
+        w_from = w_raw[:].rearrange("p j (m t) -> p m j t", t=PACK)
+        nc.scalar.copy(out=w_to[:, :, :, 0:2], in_=w_from[:, :, :, 0:2])
+        nc.scalar.copy(out=w_to[:, 0:SCALAR_CASTS, :, 2:4], in_=w_from[:, 0:SCALAR_CASTS, :, 2:4])
+        nc.vector.tensor_copy(out=w_to[:, SCALAR_CASTS:P, :, 2:4], in_=w_from[:, SCALAR_CASTS:P, :, 2:4])
         ha_g = after_w.tile([P, U], F32, align_bytes=64, offset=0)
         nc.scalar.activation(ha_g[:], ha_win[:].indirect(sv_t[:]), ACT.Copy, scale=-1.0)
         w_q = keep.tile([P, H], U32, align_bytes=64)
         w_s = keep.tile([P, H], U8, align_bytes=64)
-        nc.vector.quantize_mx(out=w_q[:].bitcast(FP8X4), scales=w_s[:], in_=w_bf[:].rearrange("p t m j -> p (t m j)"))
+        for g in range(2):
+            cols = slice(g * H // 2, (g + 1) * H // 2)
+            nc.vector.quantize_mx(
+                out=w_q[:, cols].bitcast(FP8X4), scales=w_s[:, cols], in_=w_bf[:, 2 * g : 2 * g + 2].rearrange("p t m j -> p (t m j)")
+            )
 
         xw_g = after_wq.tile([P, S], U32, align_bytes=64, offset=0)
         for i in range(TB):
@@ -128,20 +133,22 @@ def tile_picked_yrbf_tanh_p_kernel(
             nc.vector.tensor_copy(ew_g[:, g * U // 2 : (g + 1) * U // 2], ew_win[:].indirect(sv_t[:, g * U // 32 : (g + 1) * U // 32]))
         ew_members = ew_g[:].rearrange("p (u w d) -> p u d w", d=D, w=4)
 
-        def deal_words(members, dealt, pieces=1):
-            for g in range(pieces):
-                us = slice(g * V // (4 * pieces), (g + 1) * V // (4 * pieces))
-                nc.vector.tensor_copy(
-                    out=dealt[:].rearrange("p (d u w) -> p u d w", w=4, u=V // 4)[:, us], in_=ew_members[:, us, members, :]
-                )
-            return [dealt[:, d * V : (d + 1) * V] for d in range(members.stop - members.start)]
+        ew_early = keep.tile([P, FIRST * V], U32, align_bytes=64)
+        ew_late = keep.tile([P, (D - FIRST) * V], U32, align_bytes=64)
 
+        def deal_words(dealt, members, g):
+            us = slice(g * V // 8, (g + 1) * V // 8)
+            nc.vector.tensor_copy(out=dealt[:].rearrange("p (d u w) -> p u d w", w=4, u=V // 4)[:, us], in_=ew_members[:, us, members, :])
 
-        ew_d = deal_words(slice(0, FIRST), keep.tile([P, FIRST * V], U32, align_bytes=64, name="ew_first"), pieces=2)
+        deal_words(ew_early, slice(0, FIRST), 0)
+        deal_words(ew_late, slice(FIRST, D), 0)
+        deal_words(ew_early, slice(0, FIRST), 1)
+        ew_d = [ew_early[:, d * V : (d + 1) * V] for d in range(FIRST)]
+        ew_d.extend(ew_late[:, d * V : (d + 1) * V] for d in range(D - FIRST))
 
         halves = [slice(0, S // 2), slice(S // 2, S)]
         h_bf = [
-            after_h.tile([P, S // 2, PACK], BF16, align_bytes=64, name="h_low", offset=0),
+            keep.tile([P, S // 2, PACK], BF16, align_bytes=64, name="h_low"),
             keep.tile([P, S // 2, PACK], BF16, align_bytes=64, name="h_high"),
         ]
         for i in range(TB):
@@ -163,7 +170,7 @@ def tile_picked_yrbf_tanh_p_kernel(
         own_ps = bank(7)
         for i in range(TB):
             nc.tensor.transpose(own_ps[:, i * P : (i + 1) * P], own_col[:, i : i + 1].to_broadcast([P, P]), ident[:])
-        consts = after_w.tile([P, S + 2 * D], F32, align_bytes=64, offset=4096)
+        consts = after_wq.tile([P, S], F32, align_bytes=64, offset=0)
         own_row = consts[:, 0:S]
         nc.scalar.copy(
             out=own_row.rearrange("p (n i) -> p n i", i=TB), in_=own_ps[:].rearrange("p (i n) -> p n i", i=TB)
@@ -173,13 +180,11 @@ def tile_picked_yrbf_tanh_p_kernel(
         h_s = keep.tile([P, S], U8, align_bytes=64)
         for c, h_half in zip(halves, h_bf):
             nc.vector.quantize_mx(out=h_q[:, c].bitcast(FP8X4), scales=h_s[:, c], in_=h_half[:].rearrange("p n t -> p (n t)"))
-        ew_d.extend(deal_words(slice(FIRST, 4), after_h.tile([P, (4 - FIRST) * V], U32, align_bytes=64, name="ew_second", offset=0)))
-        ew_d.extend(deal_words(slice(4, D), after_h.tile([P, 4 * V], U32, align_bytes=64, name="ew_high", offset=1024)))
+        deal_words(ew_late, slice(FIRST, D), 1)
 
-        def second_product(d, c, b):
-            y_ps = bank(b)
+        def second_product(d, c, y_ps):
             nc.tensor.matmul_mx(
-                out=y_ps[:, c],
+                out=y_ps,
                 lhsT=ew_d[d].bitcast(FP8X4),
                 lhsT_scale=es_p[:, d * V : (d + 1) * V],
                 rhs=h_q[:, c].bitcast(FP8X4),
@@ -187,7 +192,6 @@ def tile_picked_yrbf_tanh_p_kernel(
                 start=True,
                 stop=True,
             )
-            return y_ps
 
         def weigh_and_add(eng, d, ee, blocks):
             c = slice(blocks[0] * P, (blocks[-1] + 1) * P)
@@ -204,18 +208,27 @@ def tile_picked_yrbf_tanh_p_kernel(
                 )
 
         whole = slice(0, S)
-        first = [second_product(0, c, b) for c, b in zip(halves, (4, 3))]
-        y_ps = [None] + [second_product(d, whole, (4 + d) % 8) for d in range(1, D - 2)]
-        ee = []
-        for d in range(D):
-            arg = work.tile([P, S], F32)
-            ee.append(work.tile([P, S], F32, name="ee"))
-            for g, c in enumerate(halves if d in (0, D - 1) else [whole]):
-                y = first[g] if d == 0 else y_ps[d]
-                nc.vector.scalar_tensor_tensor(arg[:, c], own_row[:, c], 2.0, y[:, c], ALU.mult, ALU.add)
-                nc.scalar.activation(ee[d][:, c], arg[:, c], ACT.Exp, bias=neg_half[:, d : d + 1], scale=0.5)
-            if d in (3, 4):
-                y_ps.append(second_product(d + 3, whole, (4 + d) % 8))
+        ee = [work.tile([P, S], F32, name="ee") for d in range(D)]
+
+        def exponential(d, c, y_ps):
+            arg = work.tile([P, S], F32, name="arg")
+            nc.vector.scalar_tensor_tensor(arg[:, c], own_row[:, c], 2.0, y_ps, ALU.mult, ALU.add)
+            nc.scalar.activation(ee[d][:, c], arg[:, c], ACT.Exp, bias=neg_half[:, d : d + 1], scale=0.5)
+
+        for c, b in zip(halves, (4, 3)):
+            y_ps = bank(b)
+            second_product(0, c, y_ps[:, c])
+            exponential(0, c, y_ps[:, c])
+        for d in range(1, D - 2):
+            y_ps = bank((4 + d) % 8)
+            second_product(d, whole, y_ps[:])
+            exponential(d, whole, y_ps[:])
+        for c, b in zip(halves, (7, 0)):
+            y_ps = bank(b)
+            for e in range(2):
+                second_product(D - 2 + e, c, y_ps[:, halves[e]])
+            for e in range(2):
+                exponential(D - 2 + e, c, y_ps[:, halves[e]])
         z_ps = [bank(2 + i) for i in range(TB)]
         for d in range(GP_TILES):
             weigh_and_add(nc.gpsimd, d, ee[d], range(TB))

@@ -23,7 +23,6 @@ HALF_ROW, ALPHA_ROW = 68, 72
 GP_TILES = 4
 CLEAR_SHARE = 1408
 FIRST = 2
-SCALAR_CASTS = 32
 X_ROW = 48
 E_ROW = P - 16
 
@@ -100,20 +99,17 @@ def tile_picked_yrbf_tanh_p_kernel(
         nc.vector.tensor_copy(es_g[:], es_win[:].indirect(sv_t[:]))
 
         w_bf = after_wq.tile([P, PACK, P, PACK], BF16, align_bytes=64, offset=0)
-        w_to = w_bf[:].rearrange("p t m j -> p m j t")
-        w_from = w_raw[:].rearrange("p j (m t) -> p m j t", t=PACK)
-        nc.scalar.copy(out=w_to[:, :, :, 0:2], in_=w_from[:, :, :, 0:2])
-        nc.scalar.copy(out=w_to[:, 0:SCALAR_CASTS, :, 2:4], in_=w_from[:, 0:SCALAR_CASTS, :, 2:4])
-        nc.vector.tensor_copy(out=w_to[:, SCALAR_CASTS:P, :, 2:4], in_=w_from[:, SCALAR_CASTS:P, :, 2:4])
-        ha_g = after_w.tile([P, U], F32, align_bytes=64, offset=0)
+        for g in range(2):
+            ms = slice(g * (P // 2), (g + 1) * (P // 2))
+            [nc.scalar.copy, nc.vector.tensor_copy][g](
+                out=w_bf[:].rearrange("p t m j -> p m j t")[:, ms],
+                in_=w_raw[:].rearrange("p j (m t) -> p m j t", t=PACK)[:, ms],
+            )
+        ha_g = keep.tile([P, U], F32, align_bytes=64)
         nc.scalar.activation(ha_g[:], ha_win[:].indirect(sv_t[:]), ACT.Copy, scale=-1.0)
         w_q = keep.tile([P, H], U32, align_bytes=64)
         w_s = keep.tile([P, H], U8, align_bytes=64)
-        for g in range(2):
-            cols = slice(g * H // 2, (g + 1) * H // 2)
-            nc.vector.quantize_mx(
-                out=w_q[:, cols].bitcast(FP8X4), scales=w_s[:, cols], in_=w_bf[:, 2 * g : 2 * g + 2].rearrange("p t m j -> p (t m j)")
-            )
+        nc.vector.quantize_mx(out=w_q[:].bitcast(FP8X4), scales=w_s[:], in_=w_bf[:].rearrange("p t m j -> p (t m j)"))
 
         xw_g = after_wq.tile([P, S], U32, align_bytes=64, offset=0)
         for i in range(TB):
@@ -170,7 +166,7 @@ def tile_picked_yrbf_tanh_p_kernel(
         own_ps = bank(7)
         for i in range(TB):
             nc.tensor.transpose(own_ps[:, i * P : (i + 1) * P], own_col[:, i : i + 1].to_broadcast([P, P]), ident[:])
-        consts = after_wq.tile([P, S], F32, align_bytes=64, offset=0)
+        consts = keep.tile([P, S], F32, align_bytes=64)
         own_row = consts[:, 0:S]
         nc.scalar.copy(
             out=own_row.rearrange("p (n i) -> p n i", i=TB), in_=own_ps[:].rearrange("p (i n) -> p n i", i=TB)
@@ -215,21 +211,21 @@ def tile_picked_yrbf_tanh_p_kernel(
             nc.vector.scalar_tensor_tensor(arg[:, c], own_row[:, c], 2.0, y_ps, ALU.mult, ALU.add)
             nc.scalar.activation(ee[d][:, c], arg[:, c], ACT.Exp, bias=neg_half[:, d : d + 1], scale=0.5)
 
-        for c, b in zip(halves, (4, 3)):
+        for c, b in zip(halves, (4, 5)):
             y_ps = bank(b)
             second_product(0, c, y_ps[:, c])
             exponential(0, c, y_ps[:, c])
         for d in range(1, D - 2):
-            y_ps = bank((4 + d) % 8)
+            y_ps = bank((6, 0, 1)[(d - 1) % 3])
             second_product(d, whole, y_ps[:])
             exponential(d, whole, y_ps[:])
-        for c, b in zip(halves, (7, 0)):
+        for c, b in zip(halves, (1, 6)):
             y_ps = bank(b)
             for e in range(2):
                 second_product(D - 2 + e, c, y_ps[:, halves[e]])
             for e in range(2):
                 exponential(D - 2 + e, c, y_ps[:, halves[e]])
-        z_ps = [bank(2 + i) for i in range(TB)]
+        z_ps = [bank(b) for b in (2, 3, 7, 4)]
         for d in range(GP_TILES):
             weigh_and_add(nc.gpsimd, d, ee[d], range(TB))
 

@@ -225,6 +225,15 @@ def tile_picked_yrbf_tanh_p_kernel(
                 second_product(D - 2 + e, c, y_ps[:, halves[e]])
             for e in range(2):
                 exponential(D - 2 + e, c, y_ps[:, halves[e]])
+        nc.tensor.matmul_mx(
+            out=bank(0)[:],
+            lhsT=w_q[:, 0:P].bitcast(FP8X4),
+            lhsT_scale=w_s[:, 0:P],
+            rhs=w_q[:].bitcast(FP8X4),
+            rhs_scale=w_s[:],
+            start=True,
+            stop=True,
+        )
         z_ps = [bank(b) for b in (2, 3, 7, 4)]
         for d in range(GP_TILES):
             weigh_and_add(nc.gpsimd, d, ee[d], range(TB))

@@ -211,22 +211,23 @@ def tile_picked_yrbf_tanh_p_kernel(
             nc.vector.scalar_tensor_tensor(arg[:, c], own_row[:, c], 2.0, y_ps, ALU.mult, ALU.add)
             nc.scalar.activation(ee[d][:, c], arg[:, c], ACT.Exp, bias=neg_half[:, d : d + 1], scale=0.5)
 
-        for c, b in zip(halves, (4, 5)):
-            y_ps = bank(b)
-            second_product(0, c, y_ps[:, c])
-            exponential(0, c, y_ps[:, c])
-        for d in range(1, D - 2):
-            y_ps = bank((6, 0, 1)[(d - 1) % 3])
+        for d in range(D // 2):
+            for g, c in enumerate(halves):
+                y_ps = bank((4 + 2 * d + g) % 8)
+                second_product(d, c, y_ps[:, c])
+                exponential(d, c, y_ps[:, c])
+        for d in range(D // 2, D - 2):
+            y_ps = bank(d - D // 2)
             second_product(d, whole, y_ps[:])
             exponential(d, whole, y_ps[:])
-        for c, b in zip(halves, (1, 6)):
+        for c, b in zip(halves, (3, 0)):
             y_ps = bank(b)
             for e in range(2):
                 second_product(D - 2 + e, c, y_ps[:, halves[e]])
             for e in range(2):
                 exponential(D - 2 + e, c, y_ps[:, halves[e]])
         nc.tensor.matmul_mx(
-            out=bank(0)[:],
+            out=bank(1)[:],
             lhsT=w_q[:, 0:P].bitcast(FP8X4),
             lhsT_scale=w_s[:, 0:P],
             rhs=w_q[:].bitcast(FP8X4),
@@ -234,7 +235,7 @@ def tile_picked_yrbf_tanh_p_kernel(
             start=True,
             stop=True,
         )
-        z_ps = [bank(b) for b in (2, 3, 7, 4)]
+        z_ps = [bank(4 + i) for i in range(TB)]
         for d in range(GP_TILES):
             weigh_and_add(nc.gpsimd, d, ee[d], range(TB))
 

@@ -23,6 +23,7 @@ HALF_ROW, ALPHA_ROW = 68, 72
 GP_TILES = 4
 CLEAR_SHARE = 1408
 FIRST = 2
+SCALAR_CASTS = 32
 X_ROW = 48
 E_ROW = P - 16
 
@@ -52,7 +53,7 @@ def tile_picked_yrbf_tanh_p_kernel(
         xs_win = after_xs.tile([P, T], U8, align_bytes=64, offset=0)
         es_win = keep.tile([P, W], U8, align_bytes=64)
         ha_win = keep.tile([P, W], F32, align_bytes=64)
-        zero = after_zero.tile([P, 32], F32, align_bytes=64, offset=0)
+        zero = after_zero.tile([P, 8], F32, align_bytes=64, offset=0)
 
         diag = keep.tile([P, P], F32)
         ident = keep.tile([P, P], F32)
@@ -66,7 +67,7 @@ def tile_picked_yrbf_tanh_p_kernel(
         nc.vector.memset(es_win[0:E_ROW, :].bitcast(I32), 0)
         nc.vector.memset(xs_p[:].bitcast(I32), 0)
         nc.scalar.copy(
-            ha_win[:, CLEAR_SHARE:W].rearrange("p (a b) -> p a b", b=32), zero[:].unsqueeze(1).to_broadcast([P, (W - CLEAR_SHARE) // 32, 32])
+            ha_win[:, CLEAR_SHARE:W].rearrange("p (a b) -> p a b", b=8), zero[:].unsqueeze(1).to_broadcast([P, (W - CLEAR_SHARE) // 8, 8])
         )
         nc.vector.memset(es_p[:].bitcast(I32), 0)
         diag_sq = after_wq.tile([P, P], F32, align_bytes=64, offset=0)
@@ -81,9 +82,7 @@ def tile_picked_yrbf_tanh_p_kernel(
         nc.sync.dma_start(out=w_raw[:], in_=w1.rearrange("(p j) c -> p j c", j=PACK))
         nc.sync.dma_start(out=ha_win[HALF_ROW : HALF_ROW + 1, :], in_=half[0:1, :])
         nc.sync.dma_start(out=ha_win[ALPHA_ROW : ALPHA_ROW + 1, :], in_=alpha[0:1, :])
-        own_col = after_zero.tile([P, TB], F32, align_bytes=64, offset=0)
-        nc.sync.dma_start(out=own_col[:], in_=own.rearrange("(p i) o -> p (i o)", i=TB))
-        xw_win = after_zero.tile([P, T], U32, align_bytes=64, offset=64)
+        xw_win = after_zero.tile([P, T], U32, align_bytes=64, offset=0)
         load_words(nc, xw_win, x_words)
 
         xs_g = keep.tile([P, S], U8, align_bytes=64)
@@ -94,22 +93,27 @@ def tile_picked_yrbf_tanh_p_kernel(
             )
         ew_win = after_xs.tile([P, W], U32, align_bytes=64, offset=64)
         load_words(nc, ew_win, e_words)
+        own_col = after_xs.tile([P, TB], F32, align_bytes=64, offset=0)
+        nc.sync.dma_start(out=own_col[:], in_=own.rearrange("(p i) o -> p (i o)", i=TB))
 
         es_g = keep.tile([P, U], U8, align_bytes=64)
         nc.vector.tensor_copy(es_g[:], es_win[:].indirect(sv_t[:]))
 
         w_bf = after_wq.tile([P, PACK, P, PACK], BF16, align_bytes=64, offset=0)
-        for g in range(2):
-            ms = slice(g * (P // 2), (g + 1) * (P // 2))
-            [nc.scalar.copy, nc.vector.tensor_copy][g](
-                out=w_bf[:].rearrange("p t m j -> p m j t")[:, ms],
-                in_=w_raw[:].rearrange("p j (m t) -> p m j t", t=PACK)[:, ms],
-            )
+        w_to = w_bf[:].rearrange("p t m j -> p m j t")
+        w_from = w_raw[:].rearrange("p j (m t) -> p m j t", t=PACK)
+        nc.scalar.copy(out=w_to[:, :, :, 0:2], in_=w_from[:, :, :, 0:2])
+        nc.scalar.copy(out=w_to[:, 0:SCALAR_CASTS, :, 2:4], in_=w_from[:, 0:SCALAR_CASTS, :, 2:4])
+        nc.vector.tensor_copy(out=w_to[:, SCALAR_CASTS:P, :, 2:4], in_=w_from[:, SCALAR_CASTS:P, :, 2:4])
         ha_g = keep.tile([P, U], F32, align_bytes=64)
         nc.scalar.activation(ha_g[:], ha_win[:].indirect(sv_t[:]), ACT.Copy, scale=-1.0)
         w_q = keep.tile([P, H], U32, align_bytes=64)
         w_s = keep.tile([P, H], U8, align_bytes=64)
-        nc.vector.quantize_mx(out=w_q[:].bitcast(FP8X4), scales=w_s[:], in_=w_bf[:].rearrange("p t m j -> p (t m j)"))
+        for g in range(2):
+            cols = slice(g * H // 2, (g + 1) * H // 2)
+            nc.vector.quantize_mx(
+                out=w_q[:, cols].bitcast(FP8X4), scales=w_s[:, cols], in_=w_bf[:, 2 * g : 2 * g + 2].rearrange("p t m j -> p (t m j)")
+            )
 
         xw_g = after_wq.tile([P, S], U32, align_bytes=64, offset=0)
         for i in range(TB):

@@ -50,9 +50,9 @@ def tile_picked_yrbf_tanh_p_kernel(
 
         offs_t = keep.tile([P, S // 16], U16)
         sv_t = keep.tile([P, U // 16], U16)
-        xs_win = after_xs.tile([P, T], U8, align_bytes=64, offset=0)
-        es_win = keep.tile([P, W], U8, align_bytes=64)
-        ha_win = keep.tile([P, W], F32, align_bytes=64)
+        xs_win = after_xs.tile([P, T], U8, align_bytes=256, offset=0)
+        es_win = keep.tile([P, W], U8, align_bytes=256)
+        ha_win = keep.tile([P, W], F32, align_bytes=256)
         zero = after_zero.tile([P, 8], F32, align_bytes=64, offset=0)
 
         diag = keep.tile([P, P], F32)
@@ -78,11 +78,11 @@ def tile_picked_yrbf_tanh_p_kernel(
         nc.sync.dma_start(out=xs_win[X_ROW : X_ROW + 16, :].bitcast(I32), in_=x_scales[0].bitcast(I32))
         nc.sync.dma_start(sv_t[:], sv)
         nc.sync.dma_start(out=es_win[E_ROW : E_ROW + 16, :].bitcast(I32), in_=e_scales[0].bitcast(I32))
-        w_raw = after_w.tile([P, PACK, H], F32, align_bytes=64, offset=0)
+        w_raw = after_w.tile([P, PACK, H], F32, align_bytes=256, offset=0)
         nc.sync.dma_start(out=w_raw[:], in_=w1.rearrange("(p j) c -> p j c", j=PACK))
         nc.sync.dma_start(out=ha_win[HALF_ROW : HALF_ROW + 1, :], in_=half[0:1, :])
         nc.sync.dma_start(out=ha_win[ALPHA_ROW : ALPHA_ROW + 1, :], in_=alpha[0:1, :])
-        xw_win = after_zero.tile([P, T], U32, align_bytes=64, offset=0)
+        xw_win = after_zero.tile([P, T], U32, align_bytes=256, offset=0)
         load_words(nc, xw_win, x_words)
 
         xs_g = keep.tile([P, S], U8, align_bytes=64)
@@ -91,7 +91,7 @@ def tile_picked_yrbf_tanh_p_kernel(
             nc.sync.dma_start(
                 out=xs_p[32 * q : 32 * q + 4, :].bitcast(I32), in_=xs_g[X_ROW + 4 * q : X_ROW + 4 * q + 4, :].bitcast(I32)
             )
-        ew_win = after_xs.tile([P, W], U32, align_bytes=64, offset=64)
+        ew_win = after_xs.tile([P, W], U32, align_bytes=256, offset=256)
         load_words(nc, ew_win, e_words)
         own_col = after_xs.tile([P, TB], F32, align_bytes=64, offset=0)
         nc.sync.dma_start(out=own_col[:], in_=own.rearrange("(p i) o -> p (i o)", i=TB))
@@ -243,7 +243,7 @@ def tile_picked_yrbf_tanh_p_kernel(
         for d in range(GP_TILES):
             weigh_and_add(nc.gpsimd, d, ee[d], range(TB))
 
-        res = keep.tile([P, TB, V], F32)
+        res = keep.tile([P, TB, V], F32, align_bytes=256)
         out_v = out.rearrange("(i p) v -> p i v", p=P)
         for g in range(2):
             blocks = range(2 * g, 2 * g + 2)

@@ -228,8 +228,18 @@ def tile_picked_yrbf_tanh_p_kernel(
             y_ps = bank(b)
             for e in range(2):
                 second_product(D - 2 + e, c, y_ps[:, halves[e]])
+            arg = work.tile([P, S], F32, name="arg")
+            nc.vector.scalar_tensor_tensor(
+                arg[:].rearrange("p (e n) -> p e n", e=2),
+                own_row[:, c].unsqueeze(1).to_broadcast([P, 2, S // 2]),
+                2.0,
+                y_ps[:].rearrange("p (e n) -> p e n", e=2),
+                ALU.mult,
+                ALU.add,
+            )
             for e in range(2):
-                exponential(D - 2 + e, c, y_ps[:, halves[e]])
+                d = D - 2 + e
+                nc.scalar.activation(ee[d][:, c], arg[:, halves[e]], ACT.Exp, bias=neg_half[:, d : d + 1], scale=0.5)
         nc.tensor.matmul_mx(
             out=bank(1)[:],
             lhsT=w_q[:, 0:P].bitcast(FP8X4),
@@ -247,9 +257,11 @@ def tile_picked_yrbf_tanh_p_kernel(
         out_v = out.rearrange("(i p) v -> p i v", p=P)
         for g in range(2):
             blocks = range(2 * g, 2 * g + 2)
-            for d in range(GP_TILES, D - 1):
+            singly = D - 1 - g
+            for d in range(GP_TILES, singly):
                 weigh_and_add(nc.vector, d, ee[d], blocks)
             for i in blocks:
-                weigh_and_add(nc.vector, D - 1, ee[D - 1], [i])
+                for d in range(singly, D):
+                    weigh_and_add(nc.vector, d, ee[d], [i])
                 nc.scalar.activation(res[:, i, :], z_ps[i][:, 0:V], ACT.Tanh, scale=-1.0)
-                nc.sync.dma_start(out=out_v[:, i, :], in_=res[:, i, :])
+                (nc.scalar if i == TB - 1 else nc.sync).dma_start(out=out_v[:, i, :], in_=res[:, i, :])

@@ -133,18 +133,17 @@ def tile_picked_yrbf_tanh_p_kernel(
             nc.vector.tensor_copy(ew_g[:, g * U // 2 : (g + 1) * U // 2], ew_win[:].indirect(sv_t[:, g * U // 32 : (g + 1) * U // 32]))
         ew_members = ew_g[:].rearrange("p (u w d) -> p u d w", d=D, w=4)
 
-        ew_early = keep.tile([P, FIRST * V], U32, align_bytes=64)
-        ew_late = keep.tile([P, (D - FIRST) * V], U32, align_bytes=64)
+        ew_dealt = keep.tile([P, U], U32, align_bytes=64)
 
-        def deal_words(dealt, members, g):
+        def deal_words(members, g):
             us = slice(g * V // 8, (g + 1) * V // 8)
-            nc.vector.tensor_copy(out=dealt[:].rearrange("p (d u w) -> p u d w", w=4, u=V // 4)[:, us], in_=ew_members[:, us, members, :])
+            nc.vector.tensor_copy(
+                out=ew_dealt[:].rearrange("p (d u w) -> p u d w", w=4, u=V // 4)[:, us, members], in_=ew_members[:, us, members, :]
+            )
 
-        deal_words(ew_early, slice(0, FIRST), 0)
-        deal_words(ew_late, slice(FIRST, D), 0)
-        deal_words(ew_early, slice(0, FIRST), 1)
-        ew_d = [ew_early[:, d * V : (d + 1) * V] for d in range(FIRST)]
-        ew_d.extend(ew_late[:, d * V : (d + 1) * V] for d in range(D - FIRST))
+        deal_words(slice(0, D), 0)
+        deal_words(slice(0, FIRST), 1)
+        ew_d = [ew_dealt[:, d * V : (d + 1) * V] for d in range(D)]
 
         halves = [slice(0, S // 2), slice(S // 2, S)]
         h_bf = [
@@ -180,7 +179,7 @@ def tile_picked_yrbf_tanh_p_kernel(
         h_s = keep.tile([P, S], U8, align_bytes=64)
         for c, h_half in zip(halves, h_bf):
             nc.vector.quantize_mx(out=h_q[:, c].bitcast(FP8X4), scales=h_s[:, c], in_=h_half[:].rearrange("p n t -> p (n t)"))
-        deal_words(ew_late, slice(FIRST, D), 1)
+        deal_words(slice(FIRST, D), 1)
 
         def second_product(d, c, y_ps):
             nc.tensor.matmul_mx(
@@ -228,18 +227,8 @@ def tile_picked_yrbf_tanh_p_kernel(
             y_ps = bank(b)
             for e in range(2):
                 second_product(D - 2 + e, c, y_ps[:, halves[e]])
-            arg = work.tile([P, S], F32, name="arg")
-            nc.vector.scalar_tensor_tensor(
-                arg[:].rearrange("p (e n) -> p e n", e=2),
-                own_row[:, c].unsqueeze(1).to_broadcast([P, 2, S // 2]),
-                2.0,
-                y_ps[:].rearrange("p (e n) -> p e n", e=2),
-                ALU.mult,
-                ALU.add,
-            )
             for e in range(2):
-                d = D - 2 + e
-                nc.scalar.activation(ee[d][:, c], arg[:, halves[e]], ACT.Exp, bias=neg_half[:, d : d + 1], scale=0.5)
+                exponential(D - 2 + e, c, y_ps[:, halves[e]])
         nc.tensor.matmul_mx(
             out=bank(1)[:],
             lhsT=w_q[:, 0:P].bitcast(FP8X4),
@@ -264,4 +253,4 @@ def tile_picked_yrbf_tanh_p_kernel(
                 for d in range(singly, D):
                     weigh_and_add(nc.vector, d, ee[d], [i])
                 nc.scalar.activation(res[:, i, :], z_ps[i][:, 0:V], ACT.Tanh, scale=-1.0)
-                (nc.scalar if i == TB - 1 else nc.sync).dma_start(out=out_v[:, i, :], in_=res[:, i, :])
+                nc.sync.dma_start(out=out_v[:, i, :], in_=res[:, i, :])

@@ -229,15 +229,6 @@ def tile_picked_yrbf_tanh_p_kernel(
                 second_product(D - 2 + e, c, y_ps[:, halves[e]])
             for e in range(2):
                 exponential(D - 2 + e, c, y_ps[:, halves[e]])
-        nc.tensor.matmul_mx(
-            out=bank(1)[:],
-            lhsT=w_q[:, 0:P].bitcast(FP8X4),
-            lhsT_scale=w_s[:, 0:P],
-            rhs=w_q[:].bitcast(FP8X4),
-            rhs_scale=w_s[:],
-            start=True,
-            stop=True,
-        )
         z_ps = [bank(4 + i) for i in range(TB)]
         for d in range(GP_TILES):
             weigh_and_add(nc.gpsimd, d, ee[d], range(TB))

from contextlib import ExitStack

import concourse.mybir as mybir

K, T, S, H, D, W, U = 512, 2048, 512, 512, 8, 2048, 1024
P = 128
PACK = 4
V = U // D
TB = S // P
FLOPS = 2 * K * H * S + 2 * H * S * U

F32 = mybir.dt.float32
BF16 = mybir.dt.bfloat16
I32 = mybir.dt.int32
U32 = mybir.dt.uint32
U16 = mybir.dt.uint16
U8 = mybir.dt.uint8
FP8X4 = mybir.dt.float8_e4m3fn_x4
ALU = mybir.AluOpType
ACT = mybir.ActivationFunctionType

HALF_ROW, ALPHA_ROW = 68, 72
GP_TILES = 4
CLEAR_SHARE = 1408
FIRST = 2
SCALAR_CASTS = 32
X_ROW = 48
E_ROW = P - 16


def load_words(nc, window, words):
    nc.sync.dma_start(out=window[:].bitcast(I32), in_=words[0].rearrange("p c r -> p (c r)").bitcast(I32))


def tile_picked_yrbf_tanh_p_kernel(
    tc, x_words, x_scales, w1, e_words, e_scales, half, own, alpha, offs, sv, out
):
    nc = tc.nc
    with ExitStack() as ctx:
        keep = ctx.enter_context(tc.tile_pool(name="keep", bufs=1))
        work = ctx.enter_context(tc.tile_pool(name="work", bufs=14))
        after_xs = ctx.enter_context(tc.tile_pool(name="after_xs", bufs=1))
        after_wq = ctx.enter_context(tc.tile_pool(name="after_wq", bufs=1))
        after_w = ctx.enter_context(tc.tile_pool(name="after_w", bufs=1))
        after_zero = ctx.enter_context(tc.tile_pool(name="after_zero", bufs=1))
        psum = ctx.enter_context(tc.psum_pool(name="psum", bufs=1))

        def bank(b):
            return psum.tile([P, 512], F32, name="bank%d" % b, tag="bank%d" % b)

        offs_t = keep.tile([P, S // 16], U16)
        sv_t = keep.tile([P, U // 16], U16)
        xs_win = after_xs.tile([P, T], U8, align_bytes=256, offset=0)
        es_win = keep.tile([P, W], U8, align_bytes=256)
        ha_win = keep.tile([P, W], F32, align_bytes=256)
        zero = after_zero.tile([P, 8], F32, align_bytes=64, offset=0)

        diag = keep.tile([P, P], F32)
        ident = keep.tile([P, P], F32)
        xs_p = keep.tile([P, S], U8, align_bytes=64)
        es_p = keep.tile([P, U], U8, align_bytes=64)
        nc.gpsimd.iota(diag[:], [[1, P]], base=0, channel_multiplier=-1, allow_small_or_imprecise_dtypes=True)
        nc.vector.memset(zero[:], 0.0)
        nc.vector.memset(ha_win[:, 0:CLEAR_SHARE], 0.0)
        nc.vector.memset(xs_win[0:X_ROW, :].bitcast(I32), 0)
        nc.vector.memset(xs_win[X_ROW + 16 : P, :].bitcast(I32), 0)
        nc.vector.memset(es_win[0:E_ROW, :].bitcast(I32), 0)
        nc.vector.memset(xs_p[:].bitcast(I32), 0)
        nc.scalar.copy(
            ha_win[:, CLEAR_SHARE:W].rearrange("p (a b) -> p a b", b=8), zero[:].unsqueeze(1).to_broadcast([P, (W - CLEAR_SHARE) // 8, 8])
        )
        nc.vector.memset(es_p[:].bitcast(I32), 0)
        diag_sq = after_wq.tile([P, P], F32, align_bytes=64, offset=0)
        nc.scalar.activation(diag_sq[:], diag[:], ACT.Square)
        nc.scalar.activation(ident[:], diag_sq[:], ACT.Relu, bias=1.0, scale=-1.0)

        nc.sync.dma_start(offs_t[:], offs)
        nc.sync.dma_start(out=xs_win[X_ROW : X_ROW + 16, :].bitcast(I32), in_=x_scales[0].bitcast(I32))
        nc.sync.dma_start(sv_t[:], sv)
        nc.sync.dma_start(out=es_win[E_ROW : E_ROW + 16, :].bitcast(I32), in_=e_scales[0].bitcast(I32))
        w_raw = after_w.tile([P, PACK, H], F32, align_bytes=256, offset=0)
        nc.sync.dma_start(out=w_raw[:], in_=w1.rearrange("(p j) c -> p j c", j=PACK))
        nc.sync.dma_start(out=ha_win[HALF_ROW : HALF_ROW + 1, :], in_=half[0:1, :])
        nc.sync.dma_start(out=ha_win[ALPHA_ROW : ALPHA_ROW + 1, :], in_=alpha[0:1, :])
        xw_win = after_zero.tile([P, T], U32, align_bytes=256, offset=0)
        load_words(nc, xw_win, x_words)

        xs_g = keep.tile([P, S], U8, align_bytes=64)
        nc.vector.tensor_copy(xs_g[:], xs_win[:].indirect(offs_t[:]))
        for q in range(4):
            nc.sync.dma_start(
                out=xs_p[32 * q : 32 * q + 4, :].bitcast(I32), in_=xs_g[X_ROW + 4 * q : X_ROW + 4 * q + 4, :].bitcast(I32)
            )
        ew_win = after_xs.tile([P, W], U32, align_bytes=256, offset=256)
        load_words(nc, ew_win, e_words)
        own_col = after_xs.tile([P, TB], F32, align_bytes=64, offset=0)
        nc.sync.dma_start(out=own_col[:], in_=own.rearrange("(p i) o -> p (i o)", i=TB))

        es_g = keep.tile([P, U], U8, align_bytes=64)
        nc.vector.tensor_copy(es_g[:], es_win[:].indirect(sv_t[:]))

        w_bf = after_wq.tile([P, PACK, P, PACK], BF16, align_bytes=64, offset=0)
        w_to = w_bf[:].rearrange("p t m j -> p m j t")
        w_from = w_raw[:].rearrange("p j (m t) -> p m j t", t=PACK)
        nc.scalar.copy(out=w_to[:, :, :, 0:2], in_=w_from[:, :, :, 0:2])
        nc.scalar.copy(out=w_to[:, 0:SCALAR_CASTS, :, 2:4], in_=w_from[:, 0:SCALAR_CASTS, :, 2:4])
        nc.vector.tensor_copy(out=w_to[:, SCALAR_CASTS:P, :, 2:4], in_=w_from[:, SCALAR_CASTS:P, :, 2:4])
        ha_g = keep.tile([P, U], F32, align_bytes=64)
        nc.scalar.activation(ha_g[:], ha_win[:].indirect(sv_t[:]), ACT.Copy, scale=-1.0)
        w_q = keep.tile([P, H], U32, align_bytes=64)
        w_s = keep.tile([P, H], U8, align_bytes=64)
        for g in range(2):
            cols = slice(g * H // 2, (g + 1) * H // 2)
            nc.vector.quantize_mx(
                out=w_q[:, cols].bitcast(FP8X4), scales=w_s[:, cols], in_=w_bf[:, 2 * g : 2 * g + 2].rearrange("p t m j -> p (t m j)")
            )

        xw_g = after_wq.tile([P, S], U32, align_bytes=64, offset=0)
        for i in range(TB):
            nc.vector.tensor_copy(xw_g[:, i * P : (i + 1) * P], xw_win[:].indirect(offs_t[:, i * P // 16 : (i + 1) * P // 16]))
        es_dealt = after_w.tile([P, U], U8, align_bytes=64, offset=7168)
        nc.vector.tensor_copy(out=es_dealt[:].rearrange("p (d v) -> p d v", v=V), in_=es_g[:].rearrange("p (v d) -> p d v", d=D))
        for q in range(4):
            nc.sync.dma_start(
                out=es_p[32 * q : 32 * q + 4, :].bitcast(I32), in_=es_dealt[E_ROW + 4 * q : E_ROW + 4 * q + 4, :].bitcast(I32)
            )
        neg_half = keep.tile([P, D], F32, align_bytes=64)
        coef = keep.tile([P, D], F32, align_bytes=64)
        nc.sync.dma_start(out=neg_half[:], in_=ha_g[HALF_ROW : HALF_ROW + 1, :])
        nc.sync.dma_start(out=coef[:], in_=ha_g[ALPHA_ROW : ALPHA_ROW + 1, :])
        ew_g = keep.tile([P, U], U32, align_bytes=64)
        for g in range(2):
            nc.vector.tensor_copy(ew_g[:, g * U // 2 : (g + 1) * U // 2], ew_win[:].indirect(sv_t[:, g * U // 32 : (g + 1) * U // 32]))
        ew_members = ew_g[:].rearrange("p (u w d) -> p u d w", d=D, w=4)

        ew_dealt = keep.tile([P, U], U32, align_bytes=64)

        def deal_words(members, g):
            us = slice(g * V // 8, (g + 1) * V // 8)
            nc.vector.tensor_copy(
                out=ew_dealt[:].rearrange("p (d u w) -> p u d w", w=4, u=V // 4)[:, us, members], in_=ew_members[:, us, members, :]
            )

        deal_words(slice(0, D), 0)
        deal_words(slice(0, FIRST), 1)
        ew_d = [ew_dealt[:, d * V : (d + 1) * V] for d in range(D)]

        halves = [slice(0, S // 2), slice(S // 2, S)]
        h_bf = [
            keep.tile([P, S // 2, PACK], BF16, align_bytes=64, name="h_low"),
            keep.tile([P, S // 2, PACK], BF16, align_bytes=64, name="h_high"),
        ]
        for i in range(TB):
            tok = slice(i * P, (i + 1) * P)
            h_ps = bank(i)
            for t in range(PACK):
                col = slice(t * P, (t + 1) * P)
                nc.tensor.matmul_mx(
                    out=h_ps[:, col],
                    lhsT=w_q[:, col].bitcast(FP8X4),
                    lhsT_scale=w_s[:, col],
                    rhs=xw_g[:, tok].bitcast(FP8X4),
                    rhs_scale=xs_p[:, tok],
                    start=True,
                    stop=True,
                )
            nc.scalar.copy(out=h_bf[i // 2][:, (i % 2) * P : (i % 2 + 1) * P, :], in_=h_ps[:].rearrange("p (t n) -> p n t", t=PACK))

        own_ps = bank(7)
        for i in range(TB):
            nc.tensor.transpose(own_ps[:, i * P : (i + 1) * P], own_col[:, i : i + 1].to_broadcast([P, P]), ident[:])
        consts = keep.tile([P, S], F32, align_bytes=64)
        own_row = consts[:, 0:S]
        nc.scalar.copy(
            out=own_row.rearrange("p (n i) -> p n i", i=TB), in_=own_ps[:].rearrange("p (i n) -> p n i", i=TB)
        )

        h_q = after_xs.tile([P, S], U32, align_bytes=64, offset=T)
        h_s = keep.tile([P, S], U8, align_bytes=64)
        for c, h_half in zip(halves, h_bf):
            nc.vector.quantize_mx(out=h_q[:, c].bitcast(FP8X4), scales=h_s[:, c], in_=h_half[:].rearrange("p n t -> p (n t)"))
        deal_words(slice(FIRST, D), 1)

        def second_product(d, c, y_ps):
            nc.tensor.matmul_mx(
                out=y_ps,
                lhsT=ew_d[d].bitcast(FP8X4),
                lhsT_scale=es_p[:, d * V : (d + 1) * V],
                rhs=h_q[:, c].bitcast(FP8X4),
                rhs_scale=h_s[:, c],
                start=True,
                stop=True,
            )

        def weigh_and_add(eng, d, ee, blocks):
            c = slice(blocks[0] * P, (blocks[-1] + 1) * P)
            gg = work.tile([P, S], F32, name="gg")
            eng.tensor_scalar(gg[:, c], ee[:, c], coef[:, d : d + 1], 0.0, ALU.mult, ALU.add)
            for i in blocks:
                nc.tensor.matmul(
                    z_ps[i][:, 0:V],
                    lhsT=gg[:, i * P : (i + 1) * P],
                    rhs=ident[:],
                    start=(d == 0),
                    stop=(d == D - 1),
                    is_transpose=True,
                )

        whole = slice(0, S)
        ee = [work.tile([P, S], F32, name="ee") for d in range(D)]

        def exponential(d, c, y_ps):
            arg = work.tile([P, S], F32, name="arg")
            nc.vector.scalar_tensor_tensor(arg[:, c], own_row[:, c], 2.0, y_ps, ALU.mult, ALU.add)
            nc.scalar.activation(ee[d][:, c], arg[:, c], ACT.Exp, bias=neg_half[:, d : d + 1], scale=0.5)

        for d in range(D // 2):
            for g, c in enumerate(halves):
                y_ps = bank((4 + 2 * d + g) % 8)
                second_product(d, c, y_ps[:, c])
                exponential(d, c, y_ps[:, c])
        for d in range(D // 2, D - 2):
            y_ps = bank(d - D // 2)
            second_product(d, whole, y_ps[:])
            exponential(d, whole, y_ps[:])
        for c, b in zip(halves, (3, 0)):
            y_ps = bank(b)
            for e in range(2):
                second_product(D - 2 + e, c, y_ps[:, halves[e]])
            for e in range(2):
                exponential(D - 2 + e, c, y_ps[:, halves[e]])
        z_ps = [bank(4 + i) for i in range(TB)]
        for d in range(GP_TILES):
            weigh_and_add(nc.gpsimd, d, ee[d], range(TB))

        res = keep.tile([P, TB, V], F32, align_bytes=256)
        out_v = out.rearrange("(i p) v -> p i v", p=P)
        for g in range(2):
            blocks = range(2 * g, 2 * g + 2)
            singly = D - 1 - g
            for d in range(GP_TILES, singly):
                weigh_and_add(nc.vector, d, ee[d], blocks)
            for i in blocks:
                for d in range(singly, D):
                    weigh_and_add(nc.vector, d, ee[d], [i])
                nc.scalar.activation(res[:, i, :], z_ps[i][:, 0:V], ACT.Tanh, scale=-1.0)
                nc.sync.dma_start(out=out_v[:, i, :], in_=res[:, i, :])
